import numpy as np
import ml_dtypes


def mxq(x, axis, fmt="e4m3"):
    dtype, down = {"e4m3": (ml_dtypes.float8_e4m3fn, 7), "e5m2": (ml_dtypes.float8_e5m2, 14)}[fmt]
    v = np.moveaxis(np.asarray(x, np.float32).astype(ml_dtypes.bfloat16).astype(np.float64), axis, -1)
    blocks = v.reshape(v.shape[:-1] + (-1, 32))
    amax = np.abs(blocks).max(-1, keepdims=True)
    byte = np.maximum(np.where(amax > 0, np.frexp(amax)[1] - 1 + 127, 0) - down, 1)
    scale = np.exp2(byte - 127.0)
    codes = (blocks / scale).astype(np.float32).astype(dtype).astype(np.float64)
    return np.moveaxis((codes * scale).reshape(v.shape), -1, axis)


WIDE = False


def mx_kscale(k):
    if not WIDE:
        return np.ones(k)
    levels = np.array([10, -10, 5, -5, 0])
    if k % 512:
        return np.exp2(np.random.permutation(np.resize(levels, k // 32))).repeat(32)
    a = np.empty((k // 512, 16))
    for p in range(k // 512):
        a[p, :8] = np.random.permutation(np.resize(levels, 8))
        for g in range(8):
            far = levels[np.abs(levels - a[p, g]) >= 10]
            a[p, g + 8] = far[np.random.randint(len(far))]
    return np.exp2(a.ravel()).repeat(32)


def f64(x):
    return np.asarray(x).astype(np.float64)


def striped(idx):
    return np.tile(idx.reshape(-1, 16).T, (8, 1)).astype(np.uint16)


def unstriped(offs):
    return offs[:16].T.reshape(-1).astype(np.int64)


def pack_weight(w):
    k, n = w.shape
    w = f64(np.asarray(w, np.float32).astype(ml_dtypes.bfloat16)).reshape(k // 32, 32, n)
    amax = np.abs(w).max(1)
    byte = np.clip(np.where(amax > 0, np.frexp(amax)[1] - 1 + 127 - 7, 1), 1, 254)
    scaled = (w * np.exp2(127.0 - byte)[:, None, :]).reshape(k, n).astype(np.float32)
    words = np.ascontiguousarray(scaled.reshape(k // 512, 128, 4, n).transpose(0, 1, 3, 2)).astype(ml_dtypes.float8_e4m3fn).view(np.uint8)
    return words, np.ascontiguousarray(byte.astype(np.uint8).reshape(k // 512, 16, n))


def unpack_weight(words, scales):
    g, p, n, _ = words.shape
    vals = np.ascontiguousarray(words).view(ml_dtypes.float8_e4m3fn).astype(np.float64) * np.repeat(np.exp2(scales.astype(np.float64) - 127.0), 8, axis=1)[..., None]
    return vals.transpose(0, 1, 3, 2).reshape(g * 512, n)


K, T, S, H, V, W, G = 512, 2048, 512, 512, 512, 2048, 1024
P = 2 ** 7


def setup_inputs():
    n = np.random.standard_normal
    s = mx_kscale(K)[:, None]
    u = mx_kscale(H)
    packed_xT = pack_weight(n((K, T)) * s)
    packed_eT = pack_weight(n((K, W)) * s)
    packed_vT = pack_weight(n((H, G)) / np.sqrt(H) / u[:, None])
    return {
        "x_words": packed_xT[0],
        "x_scales": packed_xT[1],
        "e_words": packed_eT[0],
        "e_scales": packed_eT[1],
        "w1": (n((K, H)) / np.sqrt(K) / s * u).astype(np.float32),
        "w2": (n((K, H)) / np.sqrt(K) / s).astype(np.float32),
        "v_words": packed_vT[0],
        "v_scales": packed_vT[1],
        "phi": (np.tile(np.random.uniform(0.0, 1.0, G), (P, 1))).astype(np.float32),
        "lift": (n((S, V))).astype(np.float32),
        "obs": (n((S, V))).astype(np.float32),
        "offs": striped(np.random.permutation(T)[:S]),
        "coef": striped(np.random.permutation(W)[:S]),
        "pts": striped(np.random.permutation(G)[:V]),
    }


def reference(x_words, x_scales, e_words, e_scales, w1, w2, v_words, v_scales, phi, lift, obs, offs, coef, pts):
    xq = unpack_weight(x_words, x_scales)[:, unstriped(offs)]
    y = mxq(f64(w1), 0, "e4m3").T @ xq
    e_coef = unpack_weight(e_words, e_scales)[:, unstriped(coef)]
    z = y * ((mxq(f64(w2), 0, "e4m3").T @ e_coef))
    v_pts = unpack_weight(v_words, v_scales)[:, unstriped(pts)]
    ss = mxq(z, 0, "e4m3").T @ v_pts
    pred = f64(lift) + ss * (f64(phi)[:1][:, unstriped(pts)])
    return (pred - f64(obs)) ** 2

@@ -1,0 +1,199 @@
+from contextlib import ExitStack
+
+import concourse.mybir as mybir
+from concourse.masks import make_identity
+
+F32 = mybir.dt.float32
+BF16 = mybir.dt.bfloat16
+I32 = mybir.dt.int32
+U32 = mybir.dt.uint32
+U16 = mybir.dt.uint16
+U8 = mybir.dt.uint8
+FP8X4 = mybir.dt.float8_e4m3fn_x4
+ALU = mybir.AluOpType
+ACT = mybir.ActivationFunctionType
+
+P = 128
+PACK = 4
+N = 512
+BLOCKS = N // P
+HALF = N // 2
+LIST_COLS = N // 16
+X_ROW, E_ROW, V_ROW = 4, 8, 12
+
+FLOPS = 3 * 2 * N * N * N
+BYTES = 2 * (2048 * 512 + 2048 * 16) + (1024 * 512 + 1024 * 16) + 5 * N * N * 4 + 1024 * 4 + 3 * P * LIST_COLS * 2
+
+
+def tile_picked_ymionet_err_p_kernel(
+    tc, x_words, x_scales, e_words, e_scales, w1, w2, v_words, v_scales, phi, lift, obs, offs, coef, pts, out
+):
+    nc = tc.nc
+    with ExitStack() as ctx:
+        keep = ctx.enter_context(tc.tile_pool(name="keep", bufs=1))
+        psum = ctx.enter_context(tc.psum_pool(name="psum", bufs=1))
+
+        def sb(name, shape, dtype):
+            return keep.tile(shape, dtype, name=name, align_bytes=64)
+
+        def load_list(name, src):
+            t = keep.tile([P, LIST_COLS], U16, name=name)
+            nc.sync.dma_start(t[:], src)
+            return t
+
+        def clear_scales(engine, name, src):
+            t = sb(name, [P, src.shape[2]], U8)
+            engine.memset(t[:].bitcast(I32), 0)
+            return t
+
+        def load_scales(queue, t, src, row):
+            rows = src[0].bitcast(I32).rearrange("(q r) c -> r q c", r=PACK)
+            for r in range(PACK):
+                queue.dma_start(t[:].bitcast(I32)[row + r : P : 32, :], rows[r])
+
+        def load_words(name, src):
+            t = sb(name, [P, src.shape[2]], I32)
+            nc.sync.dma_start(t[:], src[0].rearrange("p n t -> p (n t)").bitcast(I32))
+            return t
+
+        def stream_tile():
+            return keep.tile([P, PACK, N], F32, name="stream", bufs=2, align_bytes=64)
+
+        def load_weight(src):
+            t = stream_tile()
+            nc.sync.dma_start(t[:], src.rearrange("(p j) c -> p j c", j=PACK))
+            return t
+
+        def load_rows(dst, src, b):
+            nc.sync.dma_start(dst, src[b * P : (b + 1) * P, :])
+            return dst
+
+        def gather(name, window, offsets, dtype):
+            t = sb(name, [P, offsets.shape[1] * 16], dtype)
+            nc.vector.tensor_copy(t[:], window.indirect(offsets))
+            return t
+
+        def cast_weight(name, raw):
+            t = sb(name, [P, PACK * N], BF16)
+            nc.scalar.copy(
+                t[:].rearrange("p (t m j) -> p m j t", t=PACK, j=PACK),
+                raw[:].rearrange("p j (m t) -> p m j t", t=PACK),
+            )
+            return t
+
+        def quantize(name, values):
+            width = values.shape[1] // PACK
+            codes = sb(name + "_codes", [P, width], U32)
+            scales = sb(name + "_scales", [P, width], U8)
+            nc.vector.quantize_mx(out=codes[:].bitcast(FP8X4), scales=scales[:], in_=values[:])
+            return codes, scales
+
+        def branch(weight, halves, scales, row, b):
+            codes, w_scales = weight
+            bank = psum.tile([P, PACK, P], F32, name="branch", bufs=4)
+            half, at = divmod(b * P, HALF)
+            for t in range(PACK):
+                nc.tensor.matmul_mx(
+                    out=bank[:, t, :],
+                    lhsT=codes[:, t * P : (t + 1) * P].bitcast(FP8X4),
+                    lhsT_scale=w_scales[:, t * P : (t + 1) * P],
+                    rhs=halves[half][:, at : at + P].bitcast(FP8X4),
+                    rhs_scale=scales[row:P, b * P : (b + 1) * P],
+                    start=True,
+                    stop=True,
+                )
+            return bank[:].rearrange("p t n -> p n t")
+
+        xs_tab = clear_scales(nc.gpsimd, "xs_tab", x_scales)
+        es_tab = clear_scales(nc.vector, "es_tab", e_scales)
+        phi_tab = sb("phi_tab", [P, phi.shape[1]], F32)
+        nc.vector.memset(phi_tab[:], 0.0)
+        vs_tab = clear_scales(nc.gpsimd, "vs_tab", v_scales)
+
+        offs_t = load_list("offs_t", offs)
+        load_scales(nc.sync, xs_tab, x_scales, X_ROW)
+        pts_t = load_list("pts_t", pts)
+        coef_t = load_list("coef_t", coef)
+        w1_raw = load_weight(w1)
+        load_scales(nc.sync, es_tab, e_scales, E_ROW)
+        nc.sync.dma_start(phi_tab[0:1, :], phi[0:1, :])
+        w2_raw = load_weight(w2)
+        load_scales(nc.sync, vs_tab, v_scales, V_ROW)
+        x_tab = load_words("x_tab", x_words)
+        v_tab = load_words("v_tab", v_words)
+        e_tab = load_words("e_tab", e_words)
+
+        ident = sb("ident", [P, P], F32)
+        make_identity(nc, ident[:])
+        warm = sb("warm", [P, 1], F32)
+        nc.scalar.activation(warm[:], ident[:, 0:1], ACT.Square)
+
+        xs = gather("xs", xs_tab[:], offs_t[:], U8)
+        es = gather("es", es_tab[:], coef_t[:], U8)
+        w1_q = quantize("w1", cast_weight("w1_bf", w1_raw))
+        w2_bf = cast_weight("w2_bf", w2_raw)
+        lift_t, obs_t = [], []
+        for pair in range(BLOCKS // 2):
+            t = stream_tile()
+            for i in range(2):
+                lift_t.append(load_rows(t[:, 2 * i, :], lift, 2 * pair + i))
+                obs_t.append(load_rows(t[:, 2 * i + 1, :], obs, 2 * pair + i))
+        phi_row = gather("phi_row", phi_tab[:], pts_t[:], F32)
+        vs = gather("vs", vs_tab[:], pts_t[:], U8)
+        hc = LIST_COLS // 2
+        xg = [gather("xg%d" % h, x_tab[:].bitcast(U32), offs_t[:, h * hc : (h + 1) * hc], U32) for h in range(2)]
+
+        phi_bank = psum.tile([P, BLOCKS, P], F32, name="back", bufs=2)
+        for c in range(BLOCKS):
+            nc.tensor.transpose(phi_bank[:, c, :], phi_row[:, c * P : (c + 1) * P], ident[:])
+        phi_col = sb("phi_col", [P, BLOCKS], F32)
+        nc.scalar.copy(phi_col[:], phi_bank[:, :, 0])
+
+        y = []
+        for b in range(BLOCKS):
+            bank = branch(w1_q, xg, xs, X_ROW, b)
+            t = sb("y%d" % b, [P, P, PACK], F32)
+            nc.scalar.copy(t[:], bank)
+            y.append(t)
+
+        vg = gather("vg", v_tab[:].bitcast(U32), pts_t[:], U32)
+        w2_q = quantize("w2", w2_bf)
+        eg = [gather("eg%d" % h, e_tab[:].bitcast(U32), coef_t[:, h * hc : (h + 1) * hc], U32) for h in range(2)]
+
+        gap = []
+        for b in range(BLOCKS):
+            t = sb("gap%d" % b, [P, N], F32)
+            nc.gpsimd.tensor_tensor(t[:], lift_t[b], obs_t[b], ALU.subtract)
+            gap.append(t)
+
+        z = []
+        for b in range(BLOCKS):
+            bank = branch(w2_q, eg, es, E_ROW, b)
+            t = sb("z%d" % b, [P, P * PACK], BF16)
+            nc.vector.tensor_tensor(t[:].rearrange("p (n t) -> p n t", t=PACK), bank, y[b][:], ALU.mult)
+            z.append(t)
+
+        for b in range(BLOCKS):
+            z_codes, z_scales = quantize("z%d" % b, z[b])
+            turned = psum.tile([P, BLOCKS, P], F32, name="turned", bufs=2)
+            for c in range(BLOCKS):
+                nc.tensor.matmul_mx(
+                    out=turned[:, c, :],
+                    lhsT=vg[:, c * P : (c + 1) * P].bitcast(FP8X4),
+                    lhsT_scale=vs[V_ROW:P, c * P : (c + 1) * P],
+                    rhs=z_codes[:].bitcast(FP8X4),
+                    rhs_scale=z_scales[:],
+                    start=True,
+                    stop=True,
+                )
+            scaled = sb("scaled%d" % b, [P, BLOCKS, P], F32)
+            for c in range(BLOCKS):
+                nc.scalar.activation(scaled[:, c, :], turned[:, c, :], ACT.Copy, scale=phi_col[:, c : c + 1])
+            back = psum.tile([P, BLOCKS, P], F32, name="back", bufs=2)
+            for c in range(BLOCKS):
+                nc.tensor.transpose(back[:, c, :], scaled[:, c, :], ident[:])
+            err = sb("err%d" % b, [P, N], F32)
+            nc.vector.tensor_tensor(err[:], back[:].rearrange("p c n -> p (c n)"), gap[b][:], ALU.add)
+            res = sb("res%d" % b, [P, N], F32)
+            nc.scalar.activation(res[:], err[:], ACT.Square)
+            nc.sync.dma_start(out[b * P : (b + 1) * P, :], res[:])

@@ -33,8 +33,8 @@ def tile_picked_ymionet_err_p_kernel(
         keep = ctx.enter_context(tc.tile_pool(name="keep", bufs=1))
         psum = ctx.enter_context(tc.psum_pool(name="psum", bufs=1))
 
-        def sb(name, shape, dtype):
-            return keep.tile(shape, dtype, name=name, align_bytes=64)
+        def sb(name, shape, dtype, tag=None, bufs=1):
+            return keep.tile(shape, dtype, name=name, tag=tag or name, bufs=bufs, align_bytes=64)
 
         def load_list(name, src):
             t = keep.tile([P, LIST_COLS], U16, name=name)
@@ -51,8 +51,8 @@ def tile_picked_ymionet_err_p_kernel(
             for r in range(PACK):
                 queue.dma_start(t[:].bitcast(I32)[row + r : P : 32, :], rows[r])
 
-        def load_words(name, src):
-            t = sb(name, [P, src.shape[2]], I32)
+        def load_words(name, src, tag=None):
+            t = sb(name, [P, src.shape[2]], I32, tag)
             nc.sync.dma_start(t[:], src[0].rearrange("p n t -> p (n t)").bitcast(I32))
             return t
 
@@ -68,36 +68,42 @@ def tile_picked_ymionet_err_p_kernel(
             nc.sync.dma_start(dst, src[b * P : (b + 1) * P, :])
             return dst
 
-        def gather(name, window, offsets, dtype):
-            t = sb(name, [P, offsets.shape[1] * 16], dtype)
+        def gather(name, window, offsets, dtype, tag=None):
+            t = sb(name, [P, N], dtype, tag)
             nc.vector.tensor_copy(t[:], window.indirect(offsets))
             return t
 
+        def gather_halves(name, window, offsets, tag):
+            t = sb(name, [P, N], U32, tag)
+            cols = LIST_COLS // 2
+            for h in range(2):
+                nc.vector.tensor_copy(t[:, h * HALF : (h + 1) * HALF], window.indirect(offsets[:, h * cols : (h + 1) * cols]))
+            return t
+
         def cast_weight(name, raw):
-            t = sb(name, [P, PACK * N], BF16)
+            t = sb(name, [P, PACK * N], BF16, name)
             nc.scalar.copy(
                 t[:].rearrange("p (t m j) -> p m j t", t=PACK, j=PACK),
                 raw[:].rearrange("p j (m t) -> p m j t", t=PACK),
             )
             return t
 
-        def quantize(name, values):
+        def quantize(name, values, tag=None):
             width = values.shape[1] // PACK
-            codes = sb(name + "_codes", [P, width], U32)
+            codes = sb(name + "_codes", [P, width], U32, tag)
             scales = sb(name + "_scales", [P, width], U8)
             nc.vector.quantize_mx(out=codes[:].bitcast(FP8X4), scales=scales[:], in_=values[:])
             return codes, scales
 
-        def branch(weight, halves, scales, row, b):
+        def branch(weight, words, scales, row, b):
             codes, w_scales = weight
             bank = psum.tile([P, PACK, P], F32, name="branch", bufs=4)
-            half, at = divmod(b * P, HALF)
             for t in range(PACK):
                 nc.tensor.matmul_mx(
                     out=bank[:, t, :],
                     lhsT=codes[:, t * P : (t + 1) * P].bitcast(FP8X4),
                     lhsT_scale=w_scales[:, t * P : (t + 1) * P],
-                    rhs=halves[half][:, at : at + P].bitcast(FP8X4),
+                    rhs=words[:, b * P : (b + 1) * P].bitcast(FP8X4),
                     rhs_scale=scales[row:P, b * P : (b + 1) * P],
                     start=True,
                     stop=True,
@@ -117,10 +123,10 @@ def tile_picked_ymionet_err_p_kernel(
         w1_raw = load_weight(w1)
         load_scales(nc.sync, es_tab, e_scales, E_ROW)
         nc.sync.dma_start(phi_tab[0:1, :], phi[0:1, :])
+        v_tab = load_words("v_tab", v_words)
         w2_raw = load_weight(w2)
         load_scales(nc.sync, vs_tab, v_scales, V_ROW)
         x_tab = load_words("x_tab", x_words)
-        v_tab = load_words("v_tab", v_words)
         e_tab = load_words("e_tab", e_words)
 
         ident = sb("ident", [P, P], F32)
@@ -139,15 +145,9 @@ def tile_picked_ymionet_err_p_kernel(
                 lift_t.append(load_rows(t[:, 2 * i, :], lift, 2 * pair + i))
                 obs_t.append(load_rows(t[:, 2 * i + 1, :], obs, 2 * pair + i))
         phi_row = gather("phi_row", phi_tab[:], pts_t[:], F32)
+        vg = gather("vg", v_tab[:].bitcast(U32), pts_t[:], U32)
         vs = gather("vs", vs_tab[:], pts_t[:], U8)
-        hc = LIST_COLS // 2
-        xg = [gather("xg%d" % h, x_tab[:].bitcast(U32), offs_t[:, h * hc : (h + 1) * hc], U32) for h in range(2)]
-
-        phi_bank = psum.tile([P, BLOCKS, P], F32, name="back", bufs=2)
-        for c in range(BLOCKS):
-            nc.tensor.transpose(phi_bank[:, c, :], phi_row[:, c * P : (c + 1) * P], ident[:])
-        phi_col = sb("phi_col", [P, BLOCKS], F32)
-        nc.scalar.copy(phi_col[:], phi_bank[:, :, 0])
+        xg = gather_halves("xg", x_tab[:].bitcast(U32), offs_t, "w1_bf")
 
         y = []
         for b in range(BLOCKS):
@@ -156,9 +156,14 @@ def tile_picked_ymionet_err_p_kernel(
             nc.scalar.copy(t[:], bank)
             y.append(t)
 
-        vg = gather("vg", v_tab[:].bitcast(U32), pts_t[:], U32)
-        w2_q = quantize("w2", w2_bf)
-        eg = [gather("eg%d" % h, e_tab[:].bitcast(U32), coef_t[:, h * hc : (h + 1) * hc], U32) for h in range(2)]
+        phi_bank = psum.tile([P, BLOCKS, P], F32, name="branch", bufs=4)
+        for c in range(BLOCKS):
+            nc.tensor.transpose(phi_bank[:, c, :], phi_row[:, c * P : (c + 1) * P], ident[:])
+        phi_col = sb("phi_col", [P, BLOCKS], F32)
+        nc.scalar.copy(phi_col[:], phi_bank[:, :, 0])
+
+        w2_q = quantize("w2", w2_bf, "x_tab")
+        eg = gather_halves("eg", e_tab[:].bitcast(U32), coef_t, "w2_bf")
 
         gap = []
         for b in range(BLOCKS):
@@ -166,15 +171,14 @@ def tile_picked_ymionet_err_p_kernel(
             nc.gpsimd.tensor_tensor(t[:], lift_t[b], obs_t[b], ALU.subtract)
             gap.append(t)
 
-        z = []
-        for b in range(BLOCKS):
+        def product(b):
             bank = branch(w2_q, eg, es, E_ROW, b)
             t = sb("z%d" % b, [P, P * PACK], BF16)
             nc.vector.tensor_tensor(t[:].rearrange("p (n t) -> p n t", t=PACK), bank, y[b][:], ALU.mult)
-            z.append(t)
+            return t
 
-        for b in range(BLOCKS):
-            z_codes, z_scales = quantize("z%d" % b, z[b])
+        def trunk(b, z):
+            z_codes, z_scales = quantize("z%d" % b, z)
             turned = psum.tile([P, BLOCKS, P], F32, name="turned", bufs=2)
             for c in range(BLOCKS):
                 nc.tensor.matmul_mx(
@@ -189,6 +193,9 @@ def tile_picked_ymionet_err_p_kernel(
             scaled = sb("scaled%d" % b, [P, BLOCKS, P], F32)
             for c in range(BLOCKS):
                 nc.scalar.activation(scaled[:, c, :], turned[:, c, :], ACT.Copy, scale=phi_col[:, c : c + 1])
+            return scaled
+
+        def finish(b, scaled):
             back = psum.tile([P, BLOCKS, P], F32, name="back", bufs=2)
             for c in range(BLOCKS):
                 nc.tensor.transpose(back[:, c, :], scaled[:, c, :], ident[:])
@@ -197,3 +204,12 @@ def tile_picked_ymionet_err_p_kernel(
             res = sb("res%d" % b, [P, N], F32)
             nc.scalar.activation(res[:], err[:], ACT.Square)
             nc.sync.dma_start(out[b * P : (b + 1) * P, :], res[:])
+
+        z, scaled = {}, {}
+        for step in range(BLOCKS + 1):
+            if step < BLOCKS:
+                z[step] = product(step)
+            if step > 0:
+                scaled[step - 1] = trunk(step - 1, z[step - 1])
+        for b in range(BLOCKS):
+            finish(b, scaled[b])

@@ -165,12 +165,6 @@ def tile_picked_ymionet_err_p_kernel(
         w2_q = quantize("w2", w2_bf, "x_tab")
         eg = gather_halves("eg", e_tab[:].bitcast(U32), coef_t, "w2_bf")
 
-        gap = []
-        for b in range(BLOCKS):
-            t = sb("gap%d" % b, [P, N], F32)
-            nc.gpsimd.tensor_tensor(t[:], lift_t[b], obs_t[b], ALU.subtract)
-            gap.append(t)
-
         def product(b):
             bank = branch(w2_q, eg, es, E_ROW, b)
             t = sb("z%d" % b, [P, P * PACK], BF16)
@@ -179,7 +173,7 @@ def tile_picked_ymionet_err_p_kernel(
 
         def trunk(b, z):
             z_codes, z_scales = quantize("z%d" % b, z)
-            turned = psum.tile([P, BLOCKS, P], F32, name="turned", bufs=2)
+            turned = psum.tile([P, BLOCKS, P], F32, name="turned", bufs=4)
             for c in range(BLOCKS):
                 nc.tensor.matmul_mx(
                     out=turned[:, c, :],
@@ -196,14 +190,20 @@ def tile_picked_ymionet_err_p_kernel(
             return scaled
 
         def finish(b, scaled):
-            back = psum.tile([P, BLOCKS, P], F32, name="back", bufs=2)
+            gap = sb("gap%d" % b, [P, N], F32, "y%d" % b)
+            nc.vector.tensor_tensor(gap[:], lift_t[b], obs_t[b], ALU.subtract)
+            back = psum.tile([P, BLOCKS, P], F32, name="branch", bufs=4)
             for c in range(BLOCKS):
                 nc.tensor.transpose(back[:, c, :], scaled[:, c, :], ident[:])
             err = sb("err%d" % b, [P, N], F32)
-            nc.vector.tensor_tensor(err[:], back[:].rearrange("p c n -> p (c n)"), gap[b][:], ALU.add)
             res = sb("res%d" % b, [P, N], F32)
-            nc.scalar.activation(res[:], err[:], ACT.Square)
-            nc.sync.dma_start(out[b * P : (b + 1) * P, :], res[:])
+            width = HALF if b == BLOCKS - 1 else N
+            for at in range(0, N, width):
+                cols = slice(at, at + width)
+                nc.vector.tensor_tensor(err[:, cols], back[:].rearrange("p c n -> p (c n)")[:, cols], gap[:, cols], ALU.add)
+                nc.scalar.activation(res[:, cols], err[:, cols], ACT.Square)
+                queue = nc.scalar if (b, at + width) == (BLOCKS - 1, N) else nc.sync
+                queue.dma_start(out[b * P : (b + 1) * P, cols], res[:, cols])
 
         z, scaled = {}, {}
         for step in range(BLOCKS + 1):

@@ -19,6 +19,7 @@ N = 512
 BLOCKS = N // P
 HALF = N // 2
 LIST_COLS = N // 16
+TURNED = 2
 X_ROW, E_ROW, V_ROW = 4, 8, 12
 
 FLOPS = 3 * 2 * N * N * N
@@ -46,9 +47,9 @@ def tile_picked_ymionet_err_p_kernel(
             engine.memset(t[:].bitcast(I32), 0)
             return t
 
-        def load_scales(queue, t, src, row):
+        def load_scales(queue, t, src, row, which=range(PACK)):
             rows = src[0].bitcast(I32).rearrange("(q r) c -> r q c", r=PACK)
-            for r in range(PACK):
+            for r in which:
                 queue.dma_start(t[:].bitcast(I32)[row + r : P : 32, :], rows[r])
 
         def load_words(name, src, tag=None):
@@ -56,24 +57,22 @@ def tile_picked_ymionet_err_p_kernel(
             nc.sync.dma_start(t[:], src[0].rearrange("p n t -> p (n t)").bitcast(I32))
             return t
 
-        def stream_tile():
-            return keep.tile([P, PACK, N], F32, name="stream", bufs=2, align_bytes=64)
-
-        def load_weight(src):
-            t = stream_tile()
+        def load_weight(name, src):
+            t = sb(name, [P, PACK, N], F32)
             nc.sync.dma_start(t[:], src.rearrange("(p j) c -> p j c", j=PACK))
             return t
 
-        def load_rows(dst, src, b):
-            nc.sync.dma_start(dst, src[b * P : (b + 1) * P, :])
-            return dst
+        def load_rows(name, src, b):
+            t = sb(name, [P, N], F32)
+            nc.sync.dma_start(t[:], src[b * P : (b + 1) * P, :])
+            return t
 
         def gather(name, window, offsets, dtype, tag=None):
             t = sb(name, [P, N], dtype, tag)
             nc.vector.tensor_copy(t[:], window.indirect(offsets))
             return t
 
-        def gather_halves(name, window, offsets, tag):
+        def gather_halves(name, window, offsets, tag=None):
             t = sb(name, [P, N], U32, tag)
             cols = LIST_COLS // 2
             for h in range(2):
@@ -95,9 +94,12 @@ def tile_picked_ymionet_err_p_kernel(
             nc.vector.quantize_mx(out=codes[:].bitcast(FP8X4), scales=scales[:], in_=values[:])
             return codes, scales
 
-        def branch(weight, words, scales, row, b):
+        def bank_tile(tag):
+            return psum.tile([P, PACK, P], F32, name="bank%d" % tag)
+
+        def branch(weight, words, scales, row, b, tag):
             codes, w_scales = weight
-            bank = psum.tile([P, PACK, P], F32, name="branch", bufs=4)
+            bank = bank_tile(tag)
             for t in range(PACK):
                 nc.tensor.matmul_mx(
                     out=bank[:, t, :],
@@ -110,106 +112,134 @@ def tile_picked_ymionet_err_p_kernel(
                 )
             return bank[:].rearrange("p t n -> p n t")
 
-        xs_tab = clear_scales(nc.gpsimd, "xs_tab", x_scales)
+        xs_tab = clear_scales(nc.vector, "xs_tab", x_scales)
         es_tab = clear_scales(nc.vector, "es_tab", e_scales)
+        vs_tab = clear_scales(nc.vector, "vs_tab", v_scales)
         phi_tab = sb("phi_tab", [P, phi.shape[1]], F32)
         nc.vector.memset(phi_tab[:], 0.0)
-        vs_tab = clear_scales(nc.gpsimd, "vs_tab", v_scales)
 
         offs_t = load_list("offs_t", offs)
-        load_scales(nc.sync, xs_tab, x_scales, X_ROW)
         pts_t = load_list("pts_t", pts)
         coef_t = load_list("coef_t", coef)
-        w1_raw = load_weight(w1)
+        load_scales(nc.sync, xs_tab, x_scales, X_ROW)
+        w1_raw = load_weight("w1_raw", w1)
         load_scales(nc.sync, es_tab, e_scales, E_ROW)
-        nc.sync.dma_start(phi_tab[0:1, :], phi[0:1, :])
-        v_tab = load_words("v_tab", v_words)
-        w2_raw = load_weight(w2)
+        w2_raw = load_weight("w2_raw", w2)
         load_scales(nc.sync, vs_tab, v_scales, V_ROW)
         x_tab = load_words("x_tab", x_words)
+        nc.sync.dma_start(phi_tab[0:1, :], phi[0:1, :])
+        v_tab = load_words("v_tab", v_words)
         e_tab = load_words("e_tab", e_words)
+        obs_t = [load_rows("obs%d" % b, obs, b) for b in range(TURNED)]
+        lift_t = [load_rows("lift%d" % b, lift, b) for b in range(TURNED)]
+        for b in range(TURNED, BLOCKS):
+            lift_t.append(load_rows("lift%d" % b, lift, b))
+            obs_t.append(load_rows("obs%d" % b, obs, b))
 
         ident = sb("ident", [P, P], F32)
         make_identity(nc, ident[:])
-        warm = sb("warm", [P, 1], F32)
-        nc.scalar.activation(warm[:], ident[:, 0:1], ACT.Square)
 
         xs = gather("xs", xs_tab[:], offs_t[:], U8)
-        es = gather("es", es_tab[:], coef_t[:], U8)
-        w1_q = quantize("w1", cast_weight("w1_bf", w1_raw))
+        es = gather("es", es_tab[:], coef_t[:], U8, "xs_tab")
+        w1_bf = cast_weight("w1_bf", w1_raw)
+        w1_q = quantize("w1", w1_bf, "es_tab")
         w2_bf = cast_weight("w2_bf", w2_raw)
-        lift_t, obs_t = [], []
-        for pair in range(BLOCKS // 2):
-            t = stream_tile()
-            for i in range(2):
-                lift_t.append(load_rows(t[:, 2 * i, :], lift, 2 * pair + i))
-                obs_t.append(load_rows(t[:, 2 * i + 1, :], obs, 2 * pair + i))
-        phi_row = gather("phi_row", phi_tab[:], pts_t[:], F32)
-        vg = gather("vg", v_tab[:].bitcast(U32), pts_t[:], U32)
-        vs = gather("vs", vs_tab[:], pts_t[:], U8)
-        xg = gather_halves("xg", x_tab[:].bitcast(U32), offs_t, "w1_bf")
+        vs = gather("vs", vs_tab[:], pts_t[:], U8, "w1_bf")
+        xg = gather_halves("xg", x_tab[:].bitcast(U32), offs_t, "vs_tab")
+        w2_q = quantize("w2", w2_bf, "x_tab")
+        phi_row = sb("phi_row", [P, N], F32, "w2_raw")
+        nc.scalar.activation(phi_row[:], phi_tab[:].indirect(pts_t[:]), ACT.Copy)
 
         y = []
         for b in range(BLOCKS):
-            bank = branch(w1_q, xg, xs, X_ROW, b)
+            bank = branch(w1_q, xg, xs, X_ROW, b, b)
             t = sb("y%d" % b, [P, P, PACK], F32)
             nc.scalar.copy(t[:], bank)
             y.append(t)
 
-        phi_bank = psum.tile([P, BLOCKS, P], F32, name="branch", bufs=4)
+        phi_bank = bank_tile(0)
         for c in range(BLOCKS):
             nc.tensor.transpose(phi_bank[:, c, :], phi_row[:, c * P : (c + 1) * P], ident[:])
         phi_col = sb("phi_col", [P, BLOCKS], F32)
         nc.scalar.copy(phi_col[:], phi_bank[:, :, 0])
 
-        w2_q = quantize("w2", w2_bf, "x_tab")
-        eg = gather_halves("eg", e_tab[:].bitcast(U32), coef_t, "w2_bf")
+        vg = gather("vg", v_tab[:].bitcast(U32), pts_t[:], U32, "w2_bf")
+        eg = gather_halves("eg", e_tab[:].bitcast(U32), coef_t, "v_tab")
+        u = [branch(w2_q, eg, es, E_ROW, b, BLOCKS + b) for b in range(BLOCKS)]
 
         def product(b):
-            bank = branch(w2_q, eg, es, E_ROW, b)
+            bank = u[b]
             t = sb("z%d" % b, [P, P * PACK], BF16)
             nc.vector.tensor_tensor(t[:].rearrange("p (n t) -> p n t", t=PACK), bank, y[b][:], ALU.mult)
             return t
 
-        def trunk(b, z):
-            z_codes, z_scales = quantize("z%d" % b, z)
-            turned = psum.tile([P, BLOCKS, P], F32, name="turned", bufs=4)
-            for c in range(BLOCKS):
-                nc.tensor.matmul_mx(
-                    out=turned[:, c, :],
-                    lhsT=vg[:, c * P : (c + 1) * P].bitcast(FP8X4),
-                    lhsT_scale=vs[V_ROW:P, c * P : (c + 1) * P],
-                    rhs=z_codes[:].bitcast(FP8X4),
-                    rhs_scale=z_scales[:],
-                    start=True,
-                    stop=True,
-                )
-            scaled = sb("scaled%d" % b, [P, BLOCKS, P], F32)
-            for c in range(BLOCKS):
-                nc.scalar.activation(scaled[:, c, :], turned[:, c, :], ACT.Copy, scale=phi_col[:, c : c + 1])
+        def turn(bank, src, chunks, start=True, stop=True):
+            for i, c in enumerate(chunks):
+                nc.tensor.matmul(bank[:, i, :], src[:, c, :], ident[:], start=start, stop=stop, is_transpose=True)
+
+        def minus_obs_turned(b):
+            bank = bank_tile(1 + b)
+            turn(bank, obs_t[b][:].rearrange("p (c n) -> p c n", n=P), range(BLOCKS))
+            t = sb("minus_obs%d" % b, [P, BLOCKS, P], F32)
+            nc.scalar.activation(t[:], bank[:], ACT.Copy, scale=-1.0)
+            return t
+
+        def pieces(b):
+            return [range(0, 2), range(2, 4)] if b == BLOCKS - 1 else [range(BLOCKS)]
+
+        def trunk(b, z_q):
+            z_codes, z_scales = z_q
+            scaled = []
+            for chunks in pieces(b):
+                turned = bank_tile((BLOCKS - 1 + b + chunks.start // 2) % BLOCKS)
+                for i, c in enumerate(chunks):
+                    nc.tensor.matmul_mx(
+                        out=turned[:, i, :],
+                        lhsT=vg[:, c * P : (c + 1) * P].bitcast(FP8X4),
+                        lhsT_scale=vs[V_ROW:P, c * P : (c + 1) * P],
+                        rhs=z_codes[:].bitcast(FP8X4),
+                        rhs_scale=z_scales[:],
+                        start=True,
+                        stop=True,
+                    )
+                t = sb("scaled%d_%d" % (b, chunks.start), [P, len(chunks), P], F32)
+                for i, c in enumerate(chunks):
+                    nc.scalar.activation(t[:, i, :], turned[:, i, :], ACT.Copy, scale=phi_col[:, c : c + 1])
+                scaled.append(t)
             return scaled
 
-        def finish(b, scaled):
-            gap = sb("gap%d" % b, [P, N], F32, "y%d" % b)
-            nc.vector.tensor_tensor(gap[:], lift_t[b], obs_t[b], ALU.subtract)
-            back = psum.tile([P, BLOCKS, P], F32, name="branch", bufs=4)
-            for c in range(BLOCKS):
-                nc.tensor.transpose(back[:, c, :], scaled[:, c, :], ident[:])
-            err = sb("err%d" % b, [P, N], F32)
-            res = sb("res%d" % b, [P, N], F32)
-            width = HALF if b == BLOCKS - 1 else N
-            for at in range(0, N, width):
-                cols = slice(at, at + width)
-                nc.vector.tensor_tensor(err[:, cols], back[:].rearrange("p c n -> p (c n)")[:, cols], gap[:, cols], ALU.add)
-                nc.scalar.activation(res[:, cols], err[:, cols], ACT.Square)
-                queue = nc.scalar if (b, at + width) == (BLOCKS - 1, N) else nc.sync
-                queue.dma_start(out[b * P : (b + 1) * P, cols], res[:, cols])
+        def turn_back(b, scaled, turned_term):
+            banks = []
+            for chunks, part in zip(pieces(b), scaled):
+                back = bank_tile((BLOCKS + b + chunks.start // 2) % (2 * BLOCKS))
+                for i, c in enumerate(chunks):
+                    if turned_term is not None:
+                        nc.tensor.matmul(back[:, i, :], turned_term[:, c, :], ident[:], start=True, stop=False, is_transpose=True)
+                    nc.tensor.matmul(back[:, i, :], part[:, i, :], ident[:], start=turned_term is None, stop=True, is_transpose=True)
+                banks.append(back)
+            return banks
 
-        z, scaled = {}, {}
-        for step in range(BLOCKS + 1):
-            if step < BLOCKS:
-                z[step] = product(step)
-            if step > 0:
-                scaled[step - 1] = trunk(step - 1, z[step - 1])
+        def finish(b, banks, natural, err):
+            for chunks, back in zip(pieces(b), banks):
+                cols = slice(chunks.start * P, chunks.stop * P)
+                width = len(chunks) * P
+                res = sb("res%d_%d" % (b, chunks.start), [P, width], F32)
+                nc.vector.tensor_tensor(err[:, cols], back[:].rearrange("p c n -> p (c n)")[:, 0:width], natural[:, cols], ALU.add)
+                nc.scalar.activation(res[:], err[:, cols], ACT.Square)
+                queue = nc.scalar if (b, chunks.stop) == (BLOCKS - 1, BLOCKS) else nc.sync
+                queue.dma_start(out[b * P : (b + 1) * P, cols], res[:])
+
+        minus_obs = {b: minus_obs_turned(b) for b in range(TURNED)}
+        z, scaled, banks = {0: product(0)}, {}, {}
         for b in range(BLOCKS):
-            finish(b, scaled[b])
+            if b + 1 < BLOCKS:
+                z[b + 1] = product(b + 1)
+            scaled[b] = trunk(b, quantize("z%d" % b, z[b]))
+            if b > 0:
+                banks[b - 1] = turn_back(b - 1, scaled[b - 1], minus_obs.get(b - 1))
+        banks[BLOCKS - 1] = turn_back(BLOCKS - 1, scaled[BLOCKS - 1], None)
+        late = sb("late", [P, 2 * BLOCKS - TURNED, N], F32, "z%d" % (BLOCKS - 1))
+        for b in range(TURNED, BLOCKS):
+            nc.gpsimd.tensor_tensor(late[:, BLOCKS + b - TURNED, :], lift_t[b][:], obs_t[b][:], ALU.subtract)
+        for b in range(BLOCKS):
+            finish(b, banks[b], lift_t[b] if b < TURNED else late[:, BLOCKS + b - TURNED, :], late[:, b, :])

@@ -19,7 +19,8 @@ N = 512
 BLOCKS = N // P
 HALF = N // 2
 LIST_COLS = N // 16
-TURNED = 2
+TURNED = 1
+LAST = BLOCKS - 1
 X_ROW, E_ROW, V_ROW = 4, 8, 12
 
 FLOPS = 3 * 2 * N * N * N
@@ -79,12 +80,13 @@ def tile_picked_ymionet_err_p_kernel(
                 nc.vector.tensor_copy(t[:, h * HALF : (h + 1) * HALF], window.indirect(offsets[:, h * cols : (h + 1) * cols]))
             return t
 
-        def cast_weight(name, raw):
+        def cast_weight(name, raw, on_vector=0):
             t = sb(name, [P, PACK * N], BF16, name)
-            nc.scalar.copy(
-                t[:].rearrange("p (t m j) -> p m j t", t=PACK, j=PACK),
-                raw[:].rearrange("p j (m t) -> p m j t", t=PACK),
-            )
+            dealt = t[:].rearrange("p (t m j) -> p m j t", t=PACK, j=PACK)
+            rows = raw[:].rearrange("p j (m t) -> p m j t", t=PACK)
+            if on_vector:
+                nc.vector.tensor_copy(dealt[:, 0:on_vector], rows[:, 0:on_vector])
+            nc.scalar.copy(dealt[:, on_vector:P], rows[:, on_vector:P])
             return t
 
         def quantize(name, values, tag=None):
@@ -121,31 +123,34 @@ def tile_picked_ymionet_err_p_kernel(
         offs_t = load_list("offs_t", offs)
         pts_t = load_list("pts_t", pts)
         coef_t = load_list("coef_t", coef)
-        load_scales(nc.sync, xs_tab, x_scales, X_ROW)
         w1_raw = load_weight("w1_raw", w1)
-        load_scales(nc.sync, es_tab, e_scales, E_ROW)
+        load_scales(nc.sync, xs_tab, x_scales, X_ROW)
+        load_scales(nc.sync, es_tab, e_scales, E_ROW, range(0, 2))
         w2_raw = load_weight("w2_raw", w2)
+        load_scales(nc.sync, es_tab, e_scales, E_ROW, range(2, 4))
         load_scales(nc.sync, vs_tab, v_scales, V_ROW)
         x_tab = load_words("x_tab", x_words)
         nc.sync.dma_start(phi_tab[0:1, :], phi[0:1, :])
         v_tab = load_words("v_tab", v_words)
         e_tab = load_words("e_tab", e_words)
-        obs_t = [load_rows("obs%d" % b, obs, b) for b in range(TURNED)]
-        lift_t = [load_rows("lift%d" % b, lift, b) for b in range(TURNED)]
-        for b in range(TURNED, BLOCKS):
-            lift_t.append(load_rows("lift%d" % b, lift, b))
-            obs_t.append(load_rows("obs%d" % b, obs, b))
+        lift_t, obs_t = {}, {}
+        for b in range(BLOCKS):
+            if b == TURNED:
+                obs_t[b] = load_rows("obs%d" % b, obs, b)
+            lift_t[b] = load_rows("lift%d" % b, lift, b)
+            if b != TURNED:
+                obs_t[b] = load_rows("obs%d" % b, obs, b)
 
         ident = sb("ident", [P, P], F32)
         make_identity(nc, ident[:])
 
+        w1_bf = cast_weight("w1_bf", w1_raw, 40)
         xs = gather("xs", xs_tab[:], offs_t[:], U8)
-        es = gather("es", es_tab[:], coef_t[:], U8, "xs_tab")
-        w1_bf = cast_weight("w1_bf", w1_raw)
-        w1_q = quantize("w1", w1_bf, "es_tab")
+        w1_q = quantize("w1", w1_bf, "xs_tab")
+        es = gather("es", es_tab[:], coef_t[:], U8)
         w2_bf = cast_weight("w2_bf", w2_raw)
-        vs = gather("vs", vs_tab[:], pts_t[:], U8, "w1_bf")
-        xg = gather_halves("xg", x_tab[:].bitcast(U32), offs_t, "vs_tab")
+        vs = gather("vs", vs_tab[:], pts_t[:], U8)
+        xg = gather_halves("xg", x_tab[:].bitcast(U32), offs_t)
         w2_q = quantize("w2", w2_bf, "x_tab")
         phi_row = sb("phi_row", [P, N], F32, "w2_raw")
         nc.scalar.activation(phi_row[:], phi_tab[:].indirect(pts_t[:]), ACT.Copy)
@@ -163,83 +168,77 @@ def tile_picked_ymionet_err_p_kernel(
         phi_col = sb("phi_col", [P, BLOCKS], F32)
         nc.scalar.copy(phi_col[:], phi_bank[:, :, 0])
 
-        vg = gather("vg", v_tab[:].bitcast(U32), pts_t[:], U32, "w2_bf")
-        eg = gather_halves("eg", e_tab[:].bitcast(U32), coef_t, "v_tab")
+        vg = gather("vg", v_tab[:].bitcast(U32), pts_t[:], U32)
+        eg = gather_halves("eg", e_tab[:].bitcast(U32), coef_t)
         u = [branch(w2_q, eg, es, E_ROW, b, BLOCKS + b) for b in range(BLOCKS)]
 
         def product(b):
-            bank = u[b]
             t = sb("z%d" % b, [P, P * PACK], BF16)
-            nc.vector.tensor_tensor(t[:].rearrange("p (n t) -> p n t", t=PACK), bank, y[b][:], ALU.mult)
+            nc.vector.tensor_tensor(t[:].rearrange("p (n t) -> p n t", t=PACK), u[b], y[b][:], ALU.mult)
             return t
 
-        def turn(bank, src, chunks, start=True, stop=True):
-            for i, c in enumerate(chunks):
-                nc.tensor.matmul(bank[:, i, :], src[:, c, :], ident[:], start=start, stop=stop, is_transpose=True)
-
-        def minus_obs_turned(b):
-            bank = bank_tile(1 + b)
-            turn(bank, obs_t[b][:].rearrange("p (c n) -> p c n", n=P), range(BLOCKS))
-            t = sb("minus_obs%d" % b, [P, BLOCKS, P], F32)
-            nc.scalar.activation(t[:], bank[:], ACT.Copy, scale=-1.0)
-            return t
-
-        def pieces(b):
-            return [range(0, 2), range(2, 4)] if b == BLOCKS - 1 else [range(BLOCKS)]
+        def turn(bank, src, start=True, stop=True):
+            count = src.shape[1]
+            for c in range(count):
+                nc.tensor.matmul(
+                    bank[:, c, :], src[:, c, :], ident[:], start=start and c == 0, stop=stop and c == count - 1, is_transpose=True
+                )
 
         def trunk(b, z_q):
             z_codes, z_scales = z_q
-            scaled = []
-            for chunks in pieces(b):
-                turned = bank_tile((BLOCKS - 1 + b + chunks.start // 2) % BLOCKS)
-                for i, c in enumerate(chunks):
-                    nc.tensor.matmul_mx(
-                        out=turned[:, i, :],
-                        lhsT=vg[:, c * P : (c + 1) * P].bitcast(FP8X4),
-                        lhsT_scale=vs[V_ROW:P, c * P : (c + 1) * P],
-                        rhs=z_codes[:].bitcast(FP8X4),
-                        rhs_scale=z_scales[:],
-                        start=True,
-                        stop=True,
-                    )
-                t = sb("scaled%d_%d" % (b, chunks.start), [P, len(chunks), P], F32)
-                for i, c in enumerate(chunks):
-                    nc.scalar.activation(t[:, i, :], turned[:, i, :], ACT.Copy, scale=phi_col[:, c : c + 1])
-                scaled.append(t)
-            return scaled
+            turned = bank_tile((BLOCKS - 1 + b) % BLOCKS)
+            for c in range(BLOCKS):
+                nc.tensor.matmul_mx(
+                    out=turned[:, c, :],
+                    lhsT=vg[:, c * P : (c + 1) * P].bitcast(FP8X4),
+                    lhsT_scale=vs[V_ROW:P, c * P : (c + 1) * P],
+                    rhs=z_codes[:].bitcast(FP8X4),
+                    rhs_scale=z_scales[:],
+                    start=True,
+                    stop=True,
+                )
+            t = sb("scaled%d" % b, [P, BLOCKS, P], F32)
+            if b == LAST:
+                nc.vector.tensor_tensor(t[:], turned[:], phi_col[:].unsqueeze(2).to_broadcast([P, BLOCKS, P]), ALU.mult)
+            else:
+                for c in range(BLOCKS):
+                    nc.scalar.activation(t[:, c, :], turned[:, c, :], ACT.Copy, scale=phi_col[:, c : c + 1])
+            return t
 
-        def turn_back(b, scaled, turned_term):
-            banks = []
-            for chunks, part in zip(pieces(b), scaled):
-                back = bank_tile((BLOCKS + b + chunks.start // 2) % (2 * BLOCKS))
-                for i, c in enumerate(chunks):
-                    if turned_term is not None:
-                        nc.tensor.matmul(back[:, i, :], turned_term[:, c, :], ident[:], start=True, stop=False, is_transpose=True)
-                    nc.tensor.matmul(back[:, i, :], part[:, i, :], ident[:], start=turned_term is None, stop=True, is_transpose=True)
-                banks.append(back)
-            return banks
-
-        def finish(b, banks, natural, err):
-            for chunks, back in zip(pieces(b), banks):
-                cols = slice(chunks.start * P, chunks.stop * P)
-                width = len(chunks) * P
-                res = sb("res%d_%d" % (b, chunks.start), [P, width], F32)
-                nc.vector.tensor_tensor(err[:, cols], back[:].rearrange("p c n -> p (c n)")[:, 0:width], natural[:, cols], ALU.add)
+        def finish(b, back, natural, err):
+            width = HALF if b == LAST else N
+            for at in range(0, N, width):
+                cols = slice(at, at + width)
+                res = sb("res%d_%d" % (b, at), [P, width], F32)
+                nc.vector.tensor_tensor(err[:, cols], back[:].rearrange("p c n -> p (c n)")[:, cols], natural[:, cols], ALU.add)
                 nc.scalar.activation(res[:], err[:, cols], ACT.Square)
-                queue = nc.scalar if (b, chunks.stop) == (BLOCKS - 1, BLOCKS) else nc.sync
+                queue = nc.scalar if (b, at + width) == (LAST, N) else nc.sync
                 queue.dma_start(out[b * P : (b + 1) * P, cols], res[:])
 
-        minus_obs = {b: minus_obs_turned(b) for b in range(TURNED)}
-        z, scaled, banks = {0: product(0)}, {}, {}
-        for b in range(BLOCKS):
+        gap0 = sb("gap0", [P, N], F32, "e_tab")
+        nc.gpsimd.tensor_tensor(gap0[:], lift_t[0][:], obs_t[0][:], ALU.subtract)
+        obs_bank = bank_tile(1)
+        turn(obs_bank, obs_t[TURNED][:].rearrange("p (c n) -> p c n", n=P))
+        minus_obs = sb("minus_obs", [P, BLOCKS, P], F32)
+        nc.scalar.activation(minus_obs[:], obs_bank[:], ACT.Copy, scale=-1.0)
+
+        z, scaled, back = {0: product(0)}, {}, {}
+        for b in range(BLOCKS + 1):
             if b + 1 < BLOCKS:
                 z[b + 1] = product(b + 1)
-            scaled[b] = trunk(b, quantize("z%d" % b, z[b]))
+            if b + 1 == TURNED:
+                back[TURNED] = bank_tile(BLOCKS + TURNED)
+                turn(back[TURNED], minus_obs, stop=False)
+            if b < BLOCKS:
+                scaled[b] = trunk(b, quantize("z%d" % b, z[b]))
             if b > 0:
-                banks[b - 1] = turn_back(b - 1, scaled[b - 1], minus_obs.get(b - 1))
-        banks[BLOCKS - 1] = turn_back(BLOCKS - 1, scaled[BLOCKS - 1], None)
-        late = sb("late", [P, 2 * BLOCKS - TURNED, N], F32, "z%d" % (BLOCKS - 1))
-        for b in range(TURNED, BLOCKS):
-            nc.gpsimd.tensor_tensor(late[:, BLOCKS + b - TURNED, :], lift_t[b][:], obs_t[b][:], ALU.subtract)
+                if b - 1 != TURNED:
+                    back[b - 1] = bank_tile(BLOCKS + b - 1)
+                turn(back[b - 1], scaled[b - 1], start=b - 1 != TURNED)
+        late = sb("late", [P, BLOCKS + 2, N], F32, "z%d" % LAST)
+        natural = {0: gap0, TURNED: lift_t[TURNED]}
+        for b in range(2, BLOCKS):
+            natural[b] = late[:, BLOCKS + b - 2, :]
+            nc.gpsimd.tensor_tensor(natural[b], lift_t[b][:], obs_t[b][:], ALU.subtract)
         for b in range(BLOCKS):
-            finish(b, banks[b], lift_t[b] if b < TURNED else late[:, BLOCKS + b - TURNED, :], late[:, b, :])
+            finish(b, back[b], natural[b], late[:, b, :])

@@ -21,6 +21,8 @@ HALF = N // 2
 LIST_COLS = N // 16
 TURNED = 1
 LAST = BLOCKS - 1
+SPREAD = 8
+X_FIRST, E_FIRST = 0, 4
 X_ROW, E_ROW, V_ROW = 4, 8, 12
 
 FLOPS = 3 * 2 * N * N * N
@@ -53,6 +55,13 @@ def tile_picked_ymionet_err_p_kernel(
             for r in which:
                 queue.dma_start(t[:].bitcast(I32)[row + r : P : 32, :], rows[r])
 
+        def load_scales_spread(t, src, first):
+            nc.sync.dma_start(t[:].bitcast(I32)[first:P:SPREAD, :], src[0].bitcast(I32))
+
+        def place_scales(dst, src, first, row):
+            for r in range(PACK):
+                nc.sync.dma_start(dst[:].bitcast(I32)[row + r : P : 32, :], src[:].bitcast(I32)[first + SPREAD * r : P : 32, :])
+
         def load_words(name, src, tag=None):
             t = sb(name, [P, src.shape[2]], I32, tag)
             nc.sync.dma_start(t[:], src[0].rearrange("p n t -> p (n t)").bitcast(I32))
@@ -80,13 +89,12 @@ def tile_picked_ymionet_err_p_kernel(
                 nc.vector.tensor_copy(t[:, h * HALF : (h + 1) * HALF], window.indirect(offsets[:, h * cols : (h + 1) * cols]))
             return t
 
-        def cast_weight(name, raw, on_vector=0):
+        def cast_weight(name, raw):
             t = sb(name, [P, PACK * N], BF16, name)
-            dealt = t[:].rearrange("p (t m j) -> p m j t", t=PACK, j=PACK)
-            rows = raw[:].rearrange("p j (m t) -> p m j t", t=PACK)
-            if on_vector:
-                nc.vector.tensor_copy(dealt[:, 0:on_vector], rows[:, 0:on_vector])
-            nc.scalar.copy(dealt[:, on_vector:P], rows[:, on_vector:P])
+            nc.scalar.copy(
+                t[:].rearrange("p (t m j) -> p m j t", t=PACK, j=PACK),
+                raw[:].rearrange("p j (m t) -> p m j t", t=PACK),
+            )
             return t
 
         def quantize(name, values, tag=None):
@@ -116,27 +124,32 @@ def tile_picked_ymionet_err_p_kernel(
 
         xs_tab = clear_scales(nc.vector, "xs_tab", x_scales)
         es_tab = clear_scales(nc.vector, "es_tab", e_scales)
-        vs_tab = clear_scales(nc.vector, "vs_tab", v_scales)
         phi_tab = sb("phi_tab", [P, phi.shape[1]], F32)
         nc.vector.memset(phi_tab[:], 0.0)
+        vs_tab = clear_scales(nc.vector, "vs_tab", v_scales)
+        xs = sb("xs", [P, N], U8)
+        nc.vector.memset(xs[:].bitcast(I32), 0)
+        es = sb("es", [P, N], U8)
+        nc.vector.memset(es[:].bitcast(I32), 0)
 
-        offs_t = load_list("offs_t", offs)
-        pts_t = load_list("pts_t", pts)
-        coef_t = load_list("coef_t", coef)
         w1_raw = load_weight("w1_raw", w1)
-        load_scales(nc.sync, xs_tab, x_scales, X_ROW)
-        load_scales(nc.sync, es_tab, e_scales, E_ROW, range(0, 2))
+        offs_t = load_list("offs_t", offs)
+        load_scales_spread(xs_tab, x_scales, X_FIRST)
+        coef_t = load_list("coef_t", coef)
+        load_scales_spread(es_tab, e_scales, E_FIRST)
+        pts_t = load_list("pts_t", pts)
+        nc.sync.dma_start(phi_tab[0:1, :], phi[0:1, :])
         w2_raw = load_weight("w2_raw", w2)
-        load_scales(nc.sync, es_tab, e_scales, E_ROW, range(2, 4))
         load_scales(nc.sync, vs_tab, v_scales, V_ROW)
         x_tab = load_words("x_tab", x_words)
-        nc.sync.dma_start(phi_tab[0:1, :], phi[0:1, :])
+        xs_rows = gather("xs_rows", xs_tab[:], offs_t[:], U8)
+        place_scales(xs, xs_rows, X_FIRST, X_ROW)
         v_tab = load_words("v_tab", v_words)
         e_tab = load_words("e_tab", e_words)
-        lift_t, obs_t = {}, {}
+        es_rows = gather("es_rows", es_tab[:], coef_t[:], U8)
+        place_scales(es, es_rows, E_FIRST, E_ROW)
+        lift_t, obs_t = {}, {TURNED: load_rows("obs%d" % TURNED, obs, TURNED)}
         for b in range(BLOCKS):
-            if b == TURNED:
-                obs_t[b] = load_rows("obs%d" % b, obs, b)
             lift_t[b] = load_rows("lift%d" % b, lift, b)
             if b != TURNED:
                 obs_t[b] = load_rows("obs%d" % b, obs, b)
@@ -144,16 +157,19 @@ def tile_picked_ymionet_err_p_kernel(
         ident = sb("ident", [P, P], F32)
         make_identity(nc, ident[:])
 
-        w1_bf = cast_weight("w1_bf", w1_raw, 40)
-        xs = gather("xs", xs_tab[:], offs_t[:], U8)
-        w1_q = quantize("w1", w1_bf, "xs_tab")
-        es = gather("es", es_tab[:], coef_t[:], U8)
+        w1_bf = cast_weight("w1_bf", w1_raw)
+        w1_q = quantize("w1", w1_bf, "es_tab")
         w2_bf = cast_weight("w2_bf", w2_raw)
         vs = gather("vs", vs_tab[:], pts_t[:], U8)
+        w2_q = quantize("w2", w2_bf, "vs_tab")
         xg = gather_halves("xg", x_tab[:].bitcast(U32), offs_t)
-        w2_q = quantize("w2", w2_bf, "x_tab")
         phi_row = sb("phi_row", [P, N], F32, "w2_raw")
         nc.scalar.activation(phi_row[:], phi_tab[:].indirect(pts_t[:]), ACT.Copy)
+        phi_bank = bank_tile(2 * BLOCKS - 1)
+        for c in range(BLOCKS):
+            nc.tensor.transpose(phi_bank[:, c, :], phi_row[:, c * P : (c + 1) * P], ident[:])
+        phi_col = sb("phi_col", [P, BLOCKS], F32)
+        nc.scalar.copy(phi_col[:], phi_bank[:, :, 0])
 
         y = []
         for b in range(BLOCKS):
@@ -161,12 +177,6 @@ def tile_picked_ymionet_err_p_kernel(
             t = sb("y%d" % b, [P, P, PACK], F32)
             nc.scalar.copy(t[:], bank)
             y.append(t)
-
-        phi_bank = bank_tile(0)
-        for c in range(BLOCKS):
-            nc.tensor.transpose(phi_bank[:, c, :], phi_row[:, c * P : (c + 1) * P], ident[:])
-        phi_col = sb("phi_col", [P, BLOCKS], F32)
-        nc.scalar.copy(phi_col[:], phi_bank[:, :, 0])
 
         vg = gather("vg", v_tab[:].bitcast(U32), pts_t[:], U32)
         eg = gather_halves("eg", e_tab[:].bitcast(U32), coef_t)
@@ -206,17 +216,17 @@ def tile_picked_ymionet_err_p_kernel(
             return t
 
         def finish(b, back, natural, err):
-            width = HALF if b == LAST else N
-            for at in range(0, N, width):
+            width = N // len(natural)
+            for at, term in zip(range(0, N, width), natural):
                 cols = slice(at, at + width)
                 res = sb("res%d_%d" % (b, at), [P, width], F32)
-                nc.vector.tensor_tensor(err[:, cols], back[:].rearrange("p c n -> p (c n)")[:, cols], natural[:, cols], ALU.add)
+                nc.vector.tensor_tensor(err[:, cols], back[:].rearrange("p c n -> p (c n)")[:, cols], term, ALU.add)
                 nc.scalar.activation(res[:], err[:, cols], ACT.Square)
                 queue = nc.scalar if (b, at + width) == (LAST, N) else nc.sync
                 queue.dma_start(out[b * P : (b + 1) * P, cols], res[:])
 
-        gap0 = sb("gap0", [P, N], F32, "e_tab")
-        nc.gpsimd.tensor_tensor(gap0[:], lift_t[0][:], obs_t[0][:], ALU.subtract)
+        gap0a = sb("gap0a", [P, HALF], F32, "e_tab")
+        nc.gpsimd.tensor_tensor(gap0a[:], lift_t[0][:, 0:HALF], obs_t[0][:, 0:HALF], ALU.subtract)
         obs_bank = bank_tile(1)
         turn(obs_bank, obs_t[TURNED][:].rearrange("p (c n) -> p c n", n=P))
         minus_obs = sb("minus_obs", [P, BLOCKS, P], F32)
@@ -231,14 +241,18 @@ def tile_picked_ymionet_err_p_kernel(
                 turn(back[TURNED], minus_obs, stop=False)
             if b < BLOCKS:
                 scaled[b] = trunk(b, quantize("z%d" % b, z[b]))
+            if b == 0:
+                gap0b = sb("gap0b", [P, HALF], F32, "z0")
+                nc.gpsimd.tensor_tensor(gap0b[:], lift_t[0][:, HALF:N], obs_t[0][:, HALF:N], ALU.subtract)
             if b > 0:
                 if b - 1 != TURNED:
                     back[b - 1] = bank_tile(BLOCKS + b - 1)
                 turn(back[b - 1], scaled[b - 1], start=b - 1 != TURNED)
         late = sb("late", [P, BLOCKS + 2, N], F32, "z%d" % LAST)
-        natural = {0: gap0, TURNED: lift_t[TURNED]}
+        natural = {0: [gap0a[:], gap0b[:]], TURNED: [lift_t[TURNED][:]]}
         for b in range(2, BLOCKS):
-            natural[b] = late[:, BLOCKS + b - 2, :]
-            nc.gpsimd.tensor_tensor(natural[b], lift_t[b][:], obs_t[b][:], ALU.subtract)
+            gap = late[:, BLOCKS + b - 2, :]
+            nc.gpsimd.tensor_tensor(gap, lift_t[b][:], obs_t[b][:], ALU.subtract)
+            natural[b] = [gap[:, 0:HALF], gap[:, HALF:N]] if b == LAST else [gap]
         for b in range(BLOCKS):
             finish(b, back[b], natural[b], late[:, b, :])

@@ -144,8 +144,8 @@ def tile_picked_ymionet_err_p_kernel(
         x_tab = load_words("x_tab", x_words)
         xs_rows = gather("xs_rows", xs_tab[:], offs_t[:], U8)
         place_scales(xs, xs_rows, X_FIRST, X_ROW)
-        v_tab = load_words("v_tab", v_words)
         e_tab = load_words("e_tab", e_words)
+        v_tab = load_words("v_tab", v_words)
         es_rows = gather("es_rows", es_tab[:], coef_t[:], U8)
         place_scales(es, es_rows, E_FIRST, E_ROW)
         lift_t, obs_t = {}, {TURNED: load_rows("obs%d" % TURNED, obs, TURNED)}
@@ -161,15 +161,10 @@ def tile_picked_ymionet_err_p_kernel(
         w1_q = quantize("w1", w1_bf, "es_tab")
         w2_bf = cast_weight("w2_bf", w2_raw)
         vs = gather("vs", vs_tab[:], pts_t[:], U8)
-        w2_q = quantize("w2", w2_bf, "vs_tab")
         xg = gather_halves("xg", x_tab[:].bitcast(U32), offs_t)
+        w2_q = quantize("w2", w2_bf, "x_tab")
         phi_row = sb("phi_row", [P, N], F32, "w2_raw")
         nc.scalar.activation(phi_row[:], phi_tab[:].indirect(pts_t[:]), ACT.Copy)
-        phi_bank = bank_tile(2 * BLOCKS - 1)
-        for c in range(BLOCKS):
-            nc.tensor.transpose(phi_bank[:, c, :], phi_row[:, c * P : (c + 1) * P], ident[:])
-        phi_col = sb("phi_col", [P, BLOCKS], F32)
-        nc.scalar.copy(phi_col[:], phi_bank[:, :, 0])
 
         y = []
         for b in range(BLOCKS):
@@ -178,13 +173,19 @@ def tile_picked_ymionet_err_p_kernel(
             nc.scalar.copy(t[:], bank)
             y.append(t)
 
-        vg = gather("vg", v_tab[:].bitcast(U32), pts_t[:], U32)
+        phi_bank = bank_tile(0)
+        for c in range(BLOCKS):
+            nc.tensor.transpose(phi_bank[:, c, :], phi_row[:, c * P : (c + 1) * P], ident[:])
+        phi_col = sb("phi_col", [P, BLOCKS], F32)
+        nc.scalar.copy(phi_col[:], phi_bank[:, :, 0])
+
         eg = gather_halves("eg", e_tab[:].bitcast(U32), coef_t)
+        vg = gather("vg", v_tab[:].bitcast(U32), pts_t[:], U32)
         u = [branch(w2_q, eg, es, E_ROW, b, BLOCKS + b) for b in range(BLOCKS)]
 
         def product(b):
-            t = sb("z%d" % b, [P, P * PACK], BF16)
-            nc.vector.tensor_tensor(t[:].rearrange("p (n t) -> p n t", t=PACK), u[b], y[b][:], ALU.mult)
+            t = sb("z%d" % b, [P, P * PACK], BF16, "z0" if b == 2 else None)
+            nc.vector.tensor_tensor(t[:].rearrange("p (n t) -> p n t", t=PACK), y[b][:], u[b], ALU.mult)
             return t
 
         def turn(bank, src, start=True, stop=True):
@@ -216,43 +217,45 @@ def tile_picked_ymionet_err_p_kernel(
             return t
 
         def finish(b, back, natural, err):
-            width = N // len(natural)
-            for at, term in zip(range(0, N, width), natural):
+            width = HALF if b == LAST else N
+            for at in range(0, N, width):
                 cols = slice(at, at + width)
                 res = sb("res%d_%d" % (b, at), [P, width], F32)
-                nc.vector.tensor_tensor(err[:, cols], back[:].rearrange("p c n -> p (c n)")[:, cols], term, ALU.add)
+                nc.vector.tensor_tensor(err[:, cols], natural[:, cols], back[:].rearrange("p c n -> p (c n)")[:, cols], ALU.add)
                 nc.scalar.activation(res[:], err[:, cols], ACT.Square)
                 queue = nc.scalar if (b, at + width) == (LAST, N) else nc.sync
                 queue.dma_start(out[b * P : (b + 1) * P, cols], res[:])
 
-        gap0a = sb("gap0a", [P, HALF], F32, "e_tab")
-        nc.gpsimd.tensor_tensor(gap0a[:], lift_t[0][:, 0:HALF], obs_t[0][:, 0:HALF], ALU.subtract)
         obs_bank = bank_tile(1)
         turn(obs_bank, obs_t[TURNED][:].rearrange("p (c n) -> p c n", n=P))
         minus_obs = sb("minus_obs", [P, BLOCKS, P], F32)
         nc.scalar.activation(minus_obs[:], obs_bank[:], ACT.Copy, scale=-1.0)
 
-        z, scaled, back = {0: product(0)}, {}, {}
-        for b in range(BLOCKS + 1):
-            if b + 1 < BLOCKS:
-                z[b + 1] = product(b + 1)
-            if b + 1 == TURNED:
+        scaled, back = {}, {}
+
+        def turn_back(b):
+            if b != TURNED:
+                back[b] = bank_tile(BLOCKS + b)
+            turn(back[b], scaled[b], start=b != TURNED)
+
+        for pair in range(0, BLOCKS, 2):
+            z = [product(pair), product(pair + 1)]
+            z_q = [quantize("z%d" % (pair + i), z[i]) for i in range(2)]
+            if pair == 0:
+                gap0 = sb("gap0", [P, N], F32, "z1")
+                nc.gpsimd.tensor_tensor(gap0[:], lift_t[0][:], obs_t[0][:], ALU.subtract)
                 back[TURNED] = bank_tile(BLOCKS + TURNED)
-                turn(back[TURNED], minus_obs, stop=False)
-            if b < BLOCKS:
-                scaled[b] = trunk(b, quantize("z%d" % b, z[b]))
-            if b == 0:
-                gap0b = sb("gap0b", [P, HALF], F32, "z0")
-                nc.gpsimd.tensor_tensor(gap0b[:], lift_t[0][:, HALF:N], obs_t[0][:, HALF:N], ALU.subtract)
-            if b > 0:
-                if b - 1 != TURNED:
-                    back[b - 1] = bank_tile(BLOCKS + b - 1)
-                turn(back[b - 1], scaled[b - 1], start=b - 1 != TURNED)
+            for i in range(2):
+                scaled[pair + i] = trunk(pair + i, z_q[i])
+                if pair + i == TURNED:
+                    turn(back[TURNED], minus_obs, stop=False)
+                if pair + i > 0:
+                    turn_back(pair + i - 1)
+        turn_back(LAST)
         late = sb("late", [P, BLOCKS + 2, N], F32, "z%d" % LAST)
-        natural = {0: [gap0a[:], gap0b[:]], TURNED: [lift_t[TURNED][:]]}
+        natural = {0: gap0, TURNED: lift_t[TURNED]}
         for b in range(2, BLOCKS):
-            gap = late[:, BLOCKS + b - 2, :]
-            nc.gpsimd.tensor_tensor(gap, lift_t[b][:], obs_t[b][:], ALU.subtract)
-            natural[b] = [gap[:, 0:HALF], gap[:, HALF:N]] if b == LAST else [gap]
+            natural[b] = late[:, BLOCKS + b - 2, :]
+            nc.gpsimd.tensor_tensor(natural[b], lift_t[b][:], obs_t[b][:], ALU.subtract)
         for b in range(BLOCKS):
             finish(b, back[b], natural[b], late[:, b, :])

@@ -20,6 +20,7 @@ BLOCKS = N // P
 HALF = N // 2
 LIST_COLS = N // 16
 TURNED = 1
+EARLY = 352
 LAST = BLOCKS - 1
 SPREAD = 8
 X_FIRST, E_FIRST = 0, 4
@@ -148,23 +149,33 @@ def tile_picked_ymionet_err_p_kernel(
         v_tab = load_words("v_tab", v_words)
         es_rows = gather("es_rows", es_tab[:], coef_t[:], U8)
         place_scales(es, es_rows, E_FIRST, E_ROW)
-        lift_t, obs_t = {}, {TURNED: load_rows("obs%d" % TURNED, obs, TURNED)}
-        for b in range(BLOCKS):
+        obs_t = {b: load_rows("obs%d" % b, obs, b) for b in range(1)}
+        lift_t = {0: load_rows("lift0", lift, 0)}
+        for b in range(1, BLOCKS):
+            obs_t[b] = load_rows("obs%d" % b, obs, b)
             lift_t[b] = load_rows("lift%d" % b, lift, b)
-            if b != TURNED:
-                obs_t[b] = load_rows("obs%d" % b, obs, b)
 
         ident = sb("ident", [P, P], F32)
         make_identity(nc, ident[:])
 
         w1_bf = cast_weight("w1_bf", w1_raw)
         w1_q = quantize("w1", w1_bf, "es_tab")
+        phi_row = sb("phi_row", [P, N], F32)
+        nc.scalar.activation(phi_row[:], phi_tab[:].indirect(pts_t[:]), ACT.Copy)
+        phi_bank = bank_tile(2 * BLOCKS - 1)
+        for c in range(BLOCKS):
+            nc.tensor.transpose(phi_bank[:, c, :], phi_row[:, c * P : (c + 1) * P], ident[:])
         w2_bf = cast_weight("w2_bf", w2_raw)
+        phi_col = sb("phi_col", [P, BLOCKS], F32, "w2_raw")
+        nc.scalar.copy(phi_col[:], phi_bank[:, :, 0])
+        spread_bank = bank_tile(2 * BLOCKS - 2)
+        for c in range(BLOCKS):
+            nc.tensor.transpose(spread_bank[:, c, :], phi_col[:, c : c + 1].to_broadcast([P, P]), ident[:])
+        phi_full = sb("phi_full", [P, N], F32)
+        nc.scalar.copy(phi_full[:], spread_bank[:].rearrange("p c n -> p (c n)"))
         vs = gather("vs", vs_tab[:], pts_t[:], U8)
         xg = gather_halves("xg", x_tab[:].bitcast(U32), offs_t)
         w2_q = quantize("w2", w2_bf, "x_tab")
-        phi_row = sb("phi_row", [P, N], F32, "w2_raw")
-        nc.scalar.activation(phi_row[:], phi_tab[:].indirect(pts_t[:]), ACT.Copy)
 
         y = []
         for b in range(BLOCKS):
@@ -173,89 +184,110 @@ def tile_picked_ymionet_err_p_kernel(
             nc.scalar.copy(t[:], bank)
             y.append(t)
 
-        phi_bank = bank_tile(0)
-        for c in range(BLOCKS):
-            nc.tensor.transpose(phi_bank[:, c, :], phi_row[:, c * P : (c + 1) * P], ident[:])
-        phi_col = sb("phi_col", [P, BLOCKS], F32)
-        nc.scalar.copy(phi_col[:], phi_bank[:, :, 0])
 
         eg = gather_halves("eg", e_tab[:].bitcast(U32), coef_t)
         vg = gather("vg", v_tab[:].bitcast(U32), pts_t[:], U32)
         u = [branch(w2_q, eg, es, E_ROW, b, BLOCKS + b) for b in range(BLOCKS)]
+
+        def chunks(t):
+            return t[:].rearrange("p (c n) -> p c n", n=P)
+
+        def turn(bank, src, start=True, stop=True):
+            for c in range(BLOCKS):
+                nc.tensor.matmul(
+                    bank[:, c, :], src[:, c, :], ident[:], start=start and c == 0, stop=stop and c == BLOCKS - 1, is_transpose=True
+                )
 
         def product(b):
             t = sb("z%d" % b, [P, P * PACK], BF16, "z0" if b == 2 else None)
             nc.vector.tensor_tensor(t[:].rearrange("p (n t) -> p n t", t=PACK), y[b][:], u[b], ALU.mult)
             return t
 
-        def turn(bank, src, start=True, stop=True):
-            count = src.shape[1]
-            for c in range(count):
-                nc.tensor.matmul(
-                    bank[:, c, :], src[:, c, :], ident[:], start=start and c == 0, stop=stop and c == count - 1, is_transpose=True
-                )
+        def negate(b):
+            t = sb("minus_obs%d" % b, [P, N], F32, None if b else "v_tab")
+            if b == 0:
+                nc.gpsimd.tensor_scalar(t[:], obs_t[b][:], -1.0, 0.0, ALU.mult, ALU.add)
+            else:
+                nc.scalar.activation(t[:], obs_t[b][:], ACT.Copy, scale=-1.0)
+            return t
 
-        def trunk(b, z_q):
-            z_codes, z_scales = z_q
-            turned = bank_tile((BLOCKS - 1 + b) % BLOCKS)
+        def boundary_turned(b, there):
+            bank = bank_tile(there)
+            turn(bank, chunks(minus_obs[b]), stop=False)
+            turn(bank, chunks(lift_t[b]), start=False)
+            turned = sb("turned%d" % b, [P, BLOCKS, P], F32)
+            nc.scalar.copy(turned[:], bank[:])
+            return turned
+
+        def trunk_turned(b, z_q, there):
+            bank = bank_tile(there)
             for c in range(BLOCKS):
                 nc.tensor.matmul_mx(
-                    out=turned[:, c, :],
+                    out=bank[:, c, :],
                     lhsT=vg[:, c * P : (c + 1) * P].bitcast(FP8X4),
                     lhsT_scale=vs[V_ROW:P, c * P : (c + 1) * P],
-                    rhs=z_codes[:].bitcast(FP8X4),
-                    rhs_scale=z_scales[:],
+                    rhs=z_q[0][:].bitcast(FP8X4),
+                    rhs_scale=z_q[1][:],
                     start=True,
                     stop=True,
                 )
             t = sb("scaled%d" % b, [P, BLOCKS, P], F32)
-            if b == LAST:
-                nc.vector.tensor_tensor(t[:], turned[:], phi_col[:].unsqueeze(2).to_broadcast([P, BLOCKS, P]), ALU.mult)
-            else:
-                for c in range(BLOCKS):
-                    nc.scalar.activation(t[:, c, :], turned[:, c, :], ACT.Copy, scale=phi_col[:, c : c + 1])
+            for c in range(BLOCKS):
+                nc.scalar.activation(t[:, c, :], bank[:, c, :], ACT.Copy, scale=phi_col[:, c : c + 1])
             return t
 
-        def finish(b, back, natural, err):
-            width = HALF if b == LAST else N
-            for at in range(0, N, width):
-                cols = slice(at, at + width)
-                res = sb("res%d_%d" % (b, at), [P, width], F32)
-                nc.vector.tensor_tensor(err[:, cols], natural[:, cols], back[:].rearrange("p c n -> p (c n)")[:, cols], ALU.add)
-                nc.scalar.activation(res[:], err[:, cols], ACT.Square)
-                queue = nc.scalar if (b, at + width) == (LAST, N) else nc.sync
-                queue.dma_start(out[b * P : (b + 1) * P, cols], res[:])
+        def trunk(z_q, there):
+            bank = bank_tile(there)
+            nc.tensor.matmul_mx(
+                out=bank[:].rearrange("p c n -> p (c n)"),
+                lhsT=z_q[0][:].bitcast(FP8X4),
+                lhsT_scale=z_q[1][:],
+                rhs=vg[:].bitcast(FP8X4),
+                rhs_scale=vs[V_ROW:P, :],
+                start=True,
+                stop=True,
+            )
+            return bank[:].rearrange("p c n -> p (c n)")
 
-        obs_bank = bank_tile(1)
-        turn(obs_bank, obs_t[TURNED][:].rearrange("p (c n) -> p c n", n=P))
-        minus_obs = sb("minus_obs", [P, BLOCKS, P], F32)
-        nc.scalar.activation(minus_obs[:], obs_bank[:], ACT.Copy, scale=-1.0)
+        def square_and_store(b, total, cols, queue):
+            res = sb("res%d_%d" % (b, cols.start), [P, cols.stop - cols.start], F32)
+            nc.scalar.activation(res[:], total[:, cols], ACT.Square)
+            queue.dma_start(out[b * P : (b + 1) * P, cols], res[:])
 
-        scaled, back = {}, {}
+        def turn_back(b, there):
+            bank = bank_tile(there)
+            first, second = (boundary[b], scaled[b]) if b == 0 else (scaled[b], boundary[b])
+            turn(bank, first, stop=False)
+            turn(bank, second, start=False)
+            return bank[:].rearrange("p c n -> p (c n)")
 
-        def turn_back(b):
-            if b != TURNED:
-                back[b] = bank_tile(BLOCKS + b)
-            turn(back[b], scaled[b], start=b != TURNED)
+        minus_obs = [negate(0), negate(1)]
+        boundary, scaled = {0: boundary_turned(0, 2)}, {}
+        z = [product(0), product(1)]
+        z_q = [quantize("z%d" % i, z[i]) for i in range(2)]
+        for b in range(2):
+            scaled[b] = trunk_turned(b, z_q[b], b)
+        boundary[1] = boundary_turned(1, 3)
+        z = [product(2), product(3)]
+        z_q = [quantize("z%d" % (2 + i), z[i]) for i in range(2)]
+        ss = [trunk(z_q[i], BLOCKS + 2 + i) for i in range(2)]
 
-        for pair in range(0, BLOCKS, 2):
-            z = [product(pair), product(pair + 1)]
-            z_q = [quantize("z%d" % (pair + i), z[i]) for i in range(2)]
-            if pair == 0:
-                gap0 = sb("gap0", [P, N], F32, "z1")
-                nc.gpsimd.tensor_tensor(gap0[:], lift_t[0][:], obs_t[0][:], ALU.subtract)
-                back[TURNED] = bank_tile(BLOCKS + TURNED)
-            for i in range(2):
-                scaled[pair + i] = trunk(pair + i, z_q[i])
-                if pair + i == TURNED:
-                    turn(back[TURNED], minus_obs, stop=False)
-                if pair + i > 0:
-                    turn_back(pair + i - 1)
-        turn_back(LAST)
-        late = sb("late", [P, BLOCKS + 2, N], F32, "z%d" % LAST)
-        natural = {0: gap0, TURNED: lift_t[TURNED]}
-        for b in range(2, BLOCKS):
-            natural[b] = late[:, BLOCKS + b - 2, :]
-            nc.gpsimd.tensor_tensor(natural[b], lift_t[b][:], obs_t[b][:], ALU.subtract)
-        for b in range(BLOCKS):
-            finish(b, back[b], natural[b], late[:, b, :])
+        gap2 = sb("gap2", [P, N], F32, "z%d" % LAST)
+        nc.vector.tensor_tensor(gap2[:], lift_t[2][:], obs_t[2][:], ALU.subtract)
+        gap3 = sb("gap3", [P, N], F32, "obs2")
+        nc.gpsimd.tensor_tensor(gap3[:], lift_t[LAST][:], obs_t[LAST][:], ALU.subtract)
+        for i in range(2):
+            scaled[2 + i] = sb("scaled%d" % (2 + i), [P, N], F32, None if i else "lift2")
+            nc.vector.tensor_tensor(scaled[2 + i][:], phi_full[:], ss[i], ALU.mult)
+
+        square_and_store(0, turn_back(0, BLOCKS), slice(0, N), nc.sync)
+        last_back = turn_back(1, BLOCKS + 1)
+        err2 = sb("err2", [P, N], F32, "obs%d" % LAST)
+        nc.vector.tensor_tensor(err2[:], scaled[2][:], gap2[:], ALU.add)
+        square_and_store(2, err2, slice(0, N), nc.sync)
+        square_and_store(1, last_back, slice(0, N), nc.sync)
+        err3 = sb("err3", [P, N], F32)
+        for at in (0, HALF):
+            cols = slice(at, at + HALF)
+            nc.vector.tensor_tensor(err3[:, cols], scaled[LAST][:, cols], gap3[:, cols], ALU.add)
+            square_and_store(LAST, err3, cols, nc.scalar if at else nc.sync)

@@ -19,12 +19,8 @@ N = 512
 BLOCKS = N // P
 HALF = N // 2
 LIST_COLS = N // 16
-TURNED = 1
-EARLY = 352
 LAST = BLOCKS - 1
 SPREAD = 8
-X_FIRST, E_FIRST = 0, 4
-X_ROW, E_ROW, V_ROW = 4, 8, 12
 
 FLOPS = 3 * 2 * N * N * N
 BYTES = 2 * (2048 * 512 + 2048 * 16) + (1024 * 512 + 1024 * 16) + 5 * N * N * 4 + 1024 * 4 + 3 * P * LIST_COLS * 2
@@ -51,26 +47,21 @@ def tile_picked_ymionet_err_p_kernel(
             engine.memset(t[:].bitcast(I32), 0)
             return t
 
-        def load_scales(queue, t, src, row, which=range(PACK)):
-            rows = src[0].bitcast(I32).rearrange("(q r) c -> r q c", r=PACK)
-            for r in which:
-                queue.dma_start(t[:].bitcast(I32)[row + r : P : 32, :], rows[r])
+        def load_scales(t, src):
+            nc.sync.dma_start(t[:].bitcast(I32)[0:P:SPREAD, :], src[0].bitcast(I32))
 
-        def load_scales_spread(t, src, first):
-            nc.sync.dma_start(t[:].bitcast(I32)[first:P:SPREAD, :], src[0].bitcast(I32))
-
-        def place_scales(dst, src, first, row):
+        def place_scales(dst, src):
             for r in range(PACK):
-                nc.sync.dma_start(dst[:].bitcast(I32)[row + r : P : 32, :], src[:].bitcast(I32)[first + SPREAD * r : P : 32, :])
+                nc.sync.dma_start(dst[:].bitcast(I32)[r:P:32, :], src[:].bitcast(I32)[SPREAD * r : P : 32, :])
 
         def load_words(name, src, tag=None):
             t = sb(name, [P, src.shape[2]], I32, tag)
             nc.sync.dma_start(t[:], src[0].rearrange("p n t -> p (n t)").bitcast(I32))
             return t
 
-        def load_weight(name, src):
+        def load_weight(name, src, queue):
             t = sb(name, [P, PACK, N], F32)
-            nc.sync.dma_start(t[:], src.rearrange("(p j) c -> p j c", j=PACK))
+            queue.dma_start(t[:], src.rearrange("(p j) c -> p j c", j=PACK))
             return t
 
         def load_rows(name, src, b):
@@ -108,7 +99,7 @@ def tile_picked_ymionet_err_p_kernel(
         def bank_tile(tag):
             return psum.tile([P, PACK, P], F32, name="bank%d" % tag)
 
-        def branch(weight, words, scales, row, b, tag):
+        def branch(weight, words, scales, b, tag):
             codes, w_scales = weight
             bank = bank_tile(tag)
             for t in range(PACK):
@@ -117,7 +108,7 @@ def tile_picked_ymionet_err_p_kernel(
                     lhsT=codes[:, t * P : (t + 1) * P].bitcast(FP8X4),
                     lhsT_scale=w_scales[:, t * P : (t + 1) * P],
                     rhs=words[:, b * P : (b + 1) * P].bitcast(FP8X4),
-                    rhs_scale=scales[row:P, b * P : (b + 1) * P],
+                    rhs_scale=scales[:, b * P : (b + 1) * P],
                     start=True,
                     stop=True,
                 )
@@ -130,30 +121,34 @@ def tile_picked_ymionet_err_p_kernel(
         vs_tab = clear_scales(nc.vector, "vs_tab", v_scales)
         xs = sb("xs", [P, N], U8)
         nc.vector.memset(xs[:].bitcast(I32), 0)
-        es = sb("es", [P, N], U8)
-        nc.vector.memset(es[:].bitcast(I32), 0)
+        planes = sb("planes", [P, 2 * N], U8)
+        nc.vector.memset(planes[:].bitcast(I32), 0)
+        es, vs = (planes[:, i * N : (i + 1) * N] for i in range(2))
 
-        w1_raw = load_weight("w1_raw", w1)
+        w1_raw = load_weight("w1_raw", w1, nc.sync)
         offs_t = load_list("offs_t", offs)
-        load_scales_spread(xs_tab, x_scales, X_FIRST)
+        load_scales(xs_tab, x_scales)
         coef_t = load_list("coef_t", coef)
-        load_scales_spread(es_tab, e_scales, E_FIRST)
+        load_scales(es_tab, e_scales)
         pts_t = load_list("pts_t", pts)
         nc.sync.dma_start(phi_tab[0:1, :], phi[0:1, :])
-        w2_raw = load_weight("w2_raw", w2)
-        load_scales(nc.sync, vs_tab, v_scales, V_ROW)
+        w2_raw = load_weight("w2_raw", w2, nc.sync)
+        load_scales(vs_tab, v_scales)
         x_tab = load_words("x_tab", x_words)
         xs_rows = gather("xs_rows", xs_tab[:], offs_t[:], U8)
-        place_scales(xs, xs_rows, X_FIRST, X_ROW)
+        place_scales(xs, xs_rows)
         e_tab = load_words("e_tab", e_words)
         v_tab = load_words("v_tab", v_words)
-        es_rows = gather("es_rows", es_tab[:], coef_t[:], U8)
-        place_scales(es, es_rows, E_FIRST, E_ROW)
-        obs_t = {b: load_rows("obs%d" % b, obs, b) for b in range(1)}
-        lift_t = {0: load_rows("lift0", lift, 0)}
-        for b in range(1, BLOCKS):
-            obs_t[b] = load_rows("obs%d" % b, obs, b)
-            lift_t[b] = load_rows("lift%d" % b, lift, b)
+        scale_rows = sb("scale_rows", [P, 2 * N], U8)
+        for i, (tab, offsets) in enumerate(((es_tab, coef_t), (vs_tab, pts_t))):
+            nc.vector.tensor_copy(scale_rows[:, i * N : (i + 1) * N], tab[:].indirect(offsets[:]))
+        place_scales(planes, scale_rows)
+        obs_t, lift_t = {}, {}
+        for tiles, name, src, b in (
+            (obs_t, "obs", obs, 0), (lift_t, "lift", lift, 0), (obs_t, "obs", obs, 1), (obs_t, "obs", obs, 2),
+            (lift_t, "lift", lift, 2), (lift_t, "lift", lift, 1), (obs_t, "obs", obs, 3), (lift_t, "lift", lift, 3),
+        ):
+            tiles[b] = load_rows("%s%d" % (name, b), src, b)
 
         ident = sb("ident", [P, P], F32)
         make_identity(nc, ident[:])
@@ -168,26 +163,25 @@ def tile_picked_ymionet_err_p_kernel(
         w2_bf = cast_weight("w2_bf", w2_raw)
         phi_col = sb("phi_col", [P, BLOCKS], F32, "w2_raw")
         nc.scalar.copy(phi_col[:], phi_bank[:, :, 0])
-        spread_bank = bank_tile(2 * BLOCKS - 2)
-        for c in range(BLOCKS):
-            nc.tensor.transpose(spread_bank[:, c, :], phi_col[:, c : c + 1].to_broadcast([P, P]), ident[:])
-        phi_full = sb("phi_full", [P, N], F32)
-        nc.scalar.copy(phi_full[:], spread_bank[:].rearrange("p c n -> p (c n)"))
-        vs = gather("vs", vs_tab[:], pts_t[:], U8)
         xg = gather_halves("xg", x_tab[:].bitcast(U32), offs_t)
         w2_q = quantize("w2", w2_bf, "x_tab")
 
         y = []
         for b in range(BLOCKS):
-            bank = branch(w1_q, xg, xs, X_ROW, b, b)
+            bank = branch(w1_q, xg, xs, b, b)
             t = sb("y%d" % b, [P, P, PACK], F32)
             nc.scalar.copy(t[:], bank)
             y.append(t)
 
+        spread_bank = bank_tile(0)
+        for c in range(BLOCKS):
+            nc.tensor.transpose(spread_bank[:, c, :], phi_col[:, c : c + 1].to_broadcast([P, P]), ident[:])
+        phi_full = sb("phi_full", [P, N], F32)
+        nc.scalar.copy(phi_full[:], spread_bank[:].rearrange("p c n -> p (c n)"))
 
         eg = gather_halves("eg", e_tab[:].bitcast(U32), coef_t)
         vg = gather("vg", v_tab[:].bitcast(U32), pts_t[:], U32)
-        u = [branch(w2_q, eg, es, E_ROW, b, BLOCKS + b) for b in range(BLOCKS)]
+        u = [branch(w2_q, eg, es, b, BLOCKS + b) for b in range(BLOCKS)]
 
         def chunks(t):
             return t[:].rearrange("p (c n) -> p c n", n=P)
@@ -225,7 +219,7 @@ def tile_picked_ymionet_err_p_kernel(
                 nc.tensor.matmul_mx(
                     out=bank[:, c, :],
                     lhsT=vg[:, c * P : (c + 1) * P].bitcast(FP8X4),
-                    lhsT_scale=vs[V_ROW:P, c * P : (c + 1) * P],
+                    lhsT_scale=vs[:, c * P : (c + 1) * P],
                     rhs=z_q[0][:].bitcast(FP8X4),
                     rhs_scale=z_q[1][:],
                     start=True,
@@ -243,7 +237,7 @@ def tile_picked_ymionet_err_p_kernel(
                 lhsT=z_q[0][:].bitcast(FP8X4),
                 lhsT_scale=z_q[1][:],
                 rhs=vg[:].bitcast(FP8X4),
-                rhs_scale=vs[V_ROW:P, :],
+                rhs_scale=vs,
                 start=True,
                 stop=True,
             )
@@ -272,12 +266,12 @@ def tile_picked_ymionet_err_p_kernel(
         z_q = [quantize("z%d" % (2 + i), z[i]) for i in range(2)]
         ss = [trunk(z_q[i], BLOCKS + 2 + i) for i in range(2)]
 
-        gap2 = sb("gap2", [P, N], F32, "z%d" % LAST)
+        gap2 = sb("gap2", [P, N], F32)
         nc.vector.tensor_tensor(gap2[:], lift_t[2][:], obs_t[2][:], ALU.subtract)
-        gap3 = sb("gap3", [P, N], F32, "obs2")
+        gap3 = sb("gap3", [P, N], F32, "z%d" % LAST)
         nc.gpsimd.tensor_tensor(gap3[:], lift_t[LAST][:], obs_t[LAST][:], ALU.subtract)
         for i in range(2):
-            scaled[2 + i] = sb("scaled%d" % (2 + i), [P, N], F32, None if i else "lift2")
+            scaled[2 + i] = sb("scaled%d" % (2 + i), [P, N], F32)
             nc.vector.tensor_tensor(scaled[2 + i][:], phi_full[:], ss[i], ALU.mult)
 
         square_and_store(0, turn_back(0, BLOCKS), slice(0, N), nc.sync)

@@ -145,8 +145,8 @@ def tile_picked_ymionet_err_p_kernel(
         place_scales(planes, scale_rows)
         obs_t, lift_t = {}, {}
         for tiles, name, src, b in (
-            (obs_t, "obs", obs, 0), (lift_t, "lift", lift, 0), (obs_t, "obs", obs, 1), (obs_t, "obs", obs, 2),
-            (lift_t, "lift", lift, 2), (lift_t, "lift", lift, 1), (obs_t, "obs", obs, 3), (lift_t, "lift", lift, 3),
+            (obs_t, "obs", obs, 0), (obs_t, "obs", obs, 1), (lift_t, "lift", lift, 0), (obs_t, "obs", obs, 2),
+            (lift_t, "lift", lift, 2), (obs_t, "obs", obs, 3), (lift_t, "lift", lift, 3), (lift_t, "lift", lift, 1),
         ):
             tiles[b] = load_rows("%s%d" % (name, b), src, b)
 
@@ -183,57 +183,27 @@ def tile_picked_ymionet_err_p_kernel(
         vg = gather("vg", v_tab[:].bitcast(U32), pts_t[:], U32)
         u = [branch(w2_q, eg, es, b, BLOCKS + b) for b in range(BLOCKS)]
 
-        def chunks(t):
-            return t[:].rearrange("p (c n) -> p c n", n=P)
+        def flat(bank):
+            return bank[:].rearrange("p c n -> p (c n)")
 
-        def turn(bank, src, start=True, stop=True):
+        def turn(bank, src, start=False, stop=False):
             for c in range(BLOCKS):
                 nc.tensor.matmul(
-                    bank[:, c, :], src[:, c, :], ident[:], start=start and c == 0, stop=stop and c == BLOCKS - 1, is_transpose=True
+                    bank[:, c, :], src[c], ident[:], start=start and c == 0, stop=stop and c == LAST, is_transpose=True
                 )
+
+        def columns(t):
+            return [t[:, c * P : (c + 1) * P] for c in range(BLOCKS)]
 
         def product(b):
             t = sb("z%d" % b, [P, P * PACK], BF16, "z0" if b == 2 else None)
             nc.vector.tensor_tensor(t[:].rearrange("p (n t) -> p n t", t=PACK), y[b][:], u[b], ALU.mult)
             return t
 
-        def negate(b):
-            t = sb("minus_obs%d" % b, [P, N], F32, None if b else "v_tab")
-            if b == 0:
-                nc.gpsimd.tensor_scalar(t[:], obs_t[b][:], -1.0, 0.0, ALU.mult, ALU.add)
-            else:
-                nc.scalar.activation(t[:], obs_t[b][:], ACT.Copy, scale=-1.0)
-            return t
-
-        def boundary_turned(b, there):
-            bank = bank_tile(there)
-            turn(bank, chunks(minus_obs[b]), stop=False)
-            turn(bank, chunks(lift_t[b]), start=False)
-            turned = sb("turned%d" % b, [P, BLOCKS, P], F32)
-            nc.scalar.copy(turned[:], bank[:])
-            return turned
-
-        def trunk_turned(b, z_q, there):
-            bank = bank_tile(there)
-            for c in range(BLOCKS):
-                nc.tensor.matmul_mx(
-                    out=bank[:, c, :],
-                    lhsT=vg[:, c * P : (c + 1) * P].bitcast(FP8X4),
-                    lhsT_scale=vs[:, c * P : (c + 1) * P],
-                    rhs=z_q[0][:].bitcast(FP8X4),
-                    rhs_scale=z_q[1][:],
-                    start=True,
-                    stop=True,
-                )
-            t = sb("scaled%d" % b, [P, BLOCKS, P], F32)
-            for c in range(BLOCKS):
-                nc.scalar.activation(t[:, c, :], bank[:, c, :], ACT.Copy, scale=phi_col[:, c : c + 1])
-            return t
-
         def trunk(z_q, there):
             bank = bank_tile(there)
             nc.tensor.matmul_mx(
-                out=bank[:].rearrange("p c n -> p (c n)"),
+                out=flat(bank),
                 lhsT=z_q[0][:].bitcast(FP8X4),
                 lhsT_scale=z_q[1][:],
                 rhs=vg[:].bitcast(FP8X4),
@@ -241,47 +211,74 @@ def tile_picked_ymionet_err_p_kernel(
                 start=True,
                 stop=True,
             )
-            return bank[:].rearrange("p c n -> p (c n)")
+            return flat(bank)
 
         def square_and_store(b, total, cols, queue):
             res = sb("res%d_%d" % (b, cols.start), [P, cols.stop - cols.start], F32)
             nc.scalar.activation(res[:], total[:, cols], ACT.Square)
             queue.dma_start(out[b * P : (b + 1) * P, cols], res[:])
 
-        def turn_back(b, there):
-            bank = bank_tile(there)
-            first, second = (boundary[b], scaled[b]) if b == 0 else (scaled[b], boundary[b])
-            turn(bank, first, stop=False)
-            turn(bank, second, start=False)
-            return bank[:].rearrange("p c n -> p (c n)")
+        minus_obs0 = sb("minus_obs0", [P, N], F32)
+        nc.gpsimd.tensor_scalar(minus_obs0[:], obs_t[0][:], -1.0, 0.0, ALU.mult, ALU.add)
+        edge = [bank_tile(2), bank_tile(3)]
+        boundary = [sb("turned%d" % j, [P, N], F32) for j in range(2)]
+        turn(edge[1], columns(obs_t[1]), start=True, stop=True)
+        nc.scalar.activation(boundary[1][:], flat(edge[1]), ACT.Copy, scale=-1.0)
+        turn(edge[0], columns(minus_obs0), start=True)
+        turn(edge[0], columns(lift_t[0]), stop=True)
+        nc.scalar.copy(boundary[0][:], flat(edge[0]))
 
-        minus_obs = [negate(0), negate(1)]
-        boundary, scaled = {0: boundary_turned(0, 2)}, {}
         z = [product(0), product(1)]
-        z_q = [quantize("z%d" % i, z[i]) for i in range(2)]
-        for b in range(2):
-            scaled[b] = trunk_turned(b, z_q[b], b)
-        boundary[1] = boundary_turned(1, 3)
+        pair_codes = sb("pair_codes", [P, HALF], U32)
+        pair_scales = sb("pair_scales", [P, HALF], U8)
+        for i in range(2):
+            cols = slice(i * P, (i + 1) * P)
+            nc.vector.quantize_mx(out=pair_codes[:, cols].bitcast(FP8X4), scales=pair_scales[:, cols], in_=z[i][:])
+        scaled = []
+        for h in range(2):
+            bank = psum.tile([P, 2, HALF], F32, name="bank%d" % h)
+            for c in range(2 * h, 2 * h + 2):
+                nc.tensor.matmul_mx(
+                    out=bank[:, c % 2, :],
+                    lhsT=vg[:, c * P : (c + 1) * P].bitcast(FP8X4),
+                    lhsT_scale=vs[:, c * P : (c + 1) * P],
+                    rhs=pair_codes[:].bitcast(FP8X4),
+                    rhs_scale=pair_scales[:],
+                    start=True,
+                    stop=True,
+                )
+            for c in range(2 * h, 2 * h + 2):
+                scaled.append(sb("scaled_chunk%d" % c, [P, HALF], F32))
+                nc.scalar.activation(scaled[c][:], bank[:, c % 2, :], ACT.Copy, scale=phi_col[:, c : c + 1])
+        back = [bank_tile(0), bank_tile(BLOCKS)]
+        turn(back[1], columns(boundary[1]), start=True)
         z = [product(2), product(3)]
         z_q = [quantize("z%d" % (2 + i), z[i]) for i in range(2)]
         ss = [trunk(z_q[i], BLOCKS + 2 + i) for i in range(2)]
-
-        gap2 = sb("gap2", [P, N], F32)
-        nc.vector.tensor_tensor(gap2[:], lift_t[2][:], obs_t[2][:], ALU.subtract)
-        gap3 = sb("gap3", [P, N], F32, "z%d" % LAST)
-        nc.gpsimd.tensor_tensor(gap3[:], lift_t[LAST][:], obs_t[LAST][:], ALU.subtract)
+        gap2 = sb("gap2", [P, N], F32, "z%d" % LAST)
+        nc.gpsimd.tensor_tensor(gap2[:], lift_t[2][:], obs_t[2][:], ALU.subtract)
+        times_phi = []
         for i in range(2):
-            scaled[2 + i] = sb("scaled%d" % (2 + i), [P, N], F32)
-            nc.vector.tensor_tensor(scaled[2 + i][:], phi_full[:], ss[i], ALU.mult)
-
-        square_and_store(0, turn_back(0, BLOCKS), slice(0, N), nc.sync)
-        last_back = turn_back(1, BLOCKS + 1)
-        err2 = sb("err2", [P, N], F32, "obs%d" % LAST)
-        nc.vector.tensor_tensor(err2[:], scaled[2][:], gap2[:], ALU.add)
+            times_phi.append(sb("times_phi%d" % i, [P, N], F32))
+            nc.vector.tensor_tensor(times_phi[i][:], phi_full[:], ss[i], ALU.mult)
+        turn(back[0], columns(boundary[0]), start=True)
+        for h in range(2):
+            for j in range(2):
+                for c in range(2 * h, 2 * h + 2):
+                    nc.tensor.matmul(
+                        back[j][:, c, :], scaled[c][:, j * P : (j + 1) * P], ident[:], start=False, stop=c == LAST, is_transpose=True
+                    )
+        square_and_store(0, flat(back[0]), slice(0, N), nc.sync)
+        err2 = sb("err2", [P, N], F32)
+        nc.vector.tensor_tensor(err2[:], times_phi[0][:], gap2[:], ALU.add)
         square_and_store(2, err2, slice(0, N), nc.sync)
-        square_and_store(1, last_back, slice(0, N), nc.sync)
+        short3 = sb("short3", [P, N], F32, "lift2")
+        nc.vector.tensor_tensor(short3[:], times_phi[1][:], obs_t[LAST][:], ALU.subtract)
+        err1 = sb("err1", [P, N], F32)
+        nc.vector.tensor_tensor(err1[:], lift_t[1][:], flat(back[1]), ALU.add)
+        square_and_store(1, err1, slice(0, N), nc.sync)
         err3 = sb("err3", [P, N], F32)
         for at in (0, HALF):
             cols = slice(at, at + HALF)
-            nc.vector.tensor_tensor(err3[:, cols], scaled[LAST][:, cols], gap3[:, cols], ALU.add)
+            nc.vector.tensor_tensor(err3[:, cols], short3[:, cols], lift_t[LAST][:, cols], ALU.add)
             square_and_store(LAST, err3, cols, nc.scalar if at else nc.sync)

@@ -234,51 +234,49 @@ def tile_picked_ymionet_err_p_kernel(
         for i in range(2):
             cols = slice(i * P, (i + 1) * P)
             nc.vector.quantize_mx(out=pair_codes[:, cols].bitcast(FP8X4), scales=pair_scales[:, cols], in_=z[i][:])
+        turned_trunk = []
+        for c, there in enumerate((0, 0, 1, BLOCKS + 1)):
+            if c != 1:
+                bank = psum.tile([P, 2, HALF], F32, name="bank%d" % there)
+            turned_trunk.append(bank[:, c % 2, :])
+            nc.tensor.matmul_mx(
+                out=turned_trunk[c],
+                lhsT=vg[:, c * P : (c + 1) * P].bitcast(FP8X4),
+                lhsT_scale=vs[:, c * P : (c + 1) * P],
+                rhs=pair_codes[:].bitcast(FP8X4),
+                rhs_scale=pair_scales[:],
+                start=True,
+                stop=True,
+            )
         scaled = []
-        for h in range(2):
-            bank = psum.tile([P, 2, HALF], F32, name="bank%d" % h)
-            for c in range(2 * h, 2 * h + 2):
-                nc.tensor.matmul_mx(
-                    out=bank[:, c % 2, :],
-                    lhsT=vg[:, c * P : (c + 1) * P].bitcast(FP8X4),
-                    lhsT_scale=vs[:, c * P : (c + 1) * P],
-                    rhs=pair_codes[:].bitcast(FP8X4),
-                    rhs_scale=pair_scales[:],
-                    start=True,
-                    stop=True,
-                )
-            for c in range(2 * h, 2 * h + 2):
-                scaled.append(sb("scaled_chunk%d" % c, [P, HALF], F32))
-                nc.scalar.activation(scaled[c][:], bank[:, c % 2, :], ACT.Copy, scale=phi_col[:, c : c + 1])
-        back = [bank_tile(0), bank_tile(BLOCKS)]
-        turn(back[1], columns(boundary[1]), start=True)
+        for c in range(LAST):
+            scaled.append(sb("scaled_chunk%d" % c, [P, HALF], F32))
+            nc.scalar.activation(scaled[c][:], turned_trunk[c], ACT.Copy, scale=phi_col[:, c : c + 1])
         z = [product(2), product(3)]
         z_q = [quantize("z%d" % (2 + i), z[i]) for i in range(2)]
         ss = [trunk(z_q[i], BLOCKS + 2 + i) for i in range(2)]
+        scaled.append(sb("scaled_chunk%d" % LAST, [P, HALF], F32, "z0"))
+        nc.vector.tensor_scalar(scaled[LAST][:], turned_trunk[LAST], phi_col[:, LAST:BLOCKS], None, ALU.mult)
         gap2 = sb("gap2", [P, N], F32, "z%d" % LAST)
         nc.gpsimd.tensor_tensor(gap2[:], lift_t[2][:], obs_t[2][:], ALU.subtract)
+        gap3 = sb("gap3", [P, N], F32)
+        nc.gpsimd.tensor_tensor(gap3[:, 0:HALF], lift_t[LAST][:, 0:HALF], obs_t[LAST][:, 0:HALF], ALU.subtract)
         times_phi = []
         for i in range(2):
             times_phi.append(sb("times_phi%d" % i, [P, N], F32))
             nc.vector.tensor_tensor(times_phi[i][:], phi_full[:], ss[i], ALU.mult)
-        turn(back[0], columns(boundary[0]), start=True)
-        for h in range(2):
-            for j in range(2):
-                for c in range(2 * h, 2 * h + 2):
-                    nc.tensor.matmul(
-                        back[j][:, c, :], scaled[c][:, j * P : (j + 1) * P], ident[:], start=False, stop=c == LAST, is_transpose=True
-                    )
+        back = [bank_tile(BLOCKS + 1), bank_tile(1)]
+        for j in range(2):
+            turn(back[j], columns(boundary[j]), start=True)
+            turn(back[j], [t[:, j * P : (j + 1) * P] for t in scaled], stop=True)
         square_and_store(0, flat(back[0]), slice(0, N), nc.sync)
-        err2 = sb("err2", [P, N], F32)
-        nc.vector.tensor_tensor(err2[:], times_phi[0][:], gap2[:], ALU.add)
-        square_and_store(2, err2, slice(0, N), nc.sync)
-        short3 = sb("short3", [P, N], F32, "lift2")
-        nc.vector.tensor_tensor(short3[:], times_phi[1][:], obs_t[LAST][:], ALU.subtract)
+        nc.vector.tensor_tensor(gap3[:, HALF:N], lift_t[LAST][:, HALF:N], obs_t[LAST][:, HALF:N], ALU.subtract)
+        for i, gap in enumerate((gap2, gap3)):
+            err = sb("err%d" % (2 + i), [P, N], F32)
+            nc.vector.tensor_tensor(err[:], times_phi[i][:], gap[:], ALU.add)
+            square_and_store(2 + i, err, slice(0, N), nc.sync)
         err1 = sb("err1", [P, N], F32)
-        nc.vector.tensor_tensor(err1[:], lift_t[1][:], flat(back[1]), ALU.add)
-        square_and_store(1, err1, slice(0, N), nc.sync)
-        err3 = sb("err3", [P, N], F32)
         for at in (0, HALF):
             cols = slice(at, at + HALF)
-            nc.vector.tensor_tensor(err3[:, cols], short3[:, cols], lift_t[LAST][:, cols], ALU.add)
-            square_and_store(LAST, err3, cols, nc.scalar if at else nc.sync)
+            nc.vector.tensor_tensor(err1[:, cols], lift_t[1][:, cols], flat(back[1])[:, cols], ALU.add)
+            square_and_store(1, err1, cols, nc.scalar if at else nc.sync)

@@ -21,6 +21,7 @@ HALF = N // 2
 LIST_COLS = N // 16
 LAST = BLOCKS - 1
 SPREAD = 8
+SCALAR_GROUPS = 96
 
 FLOPS = 3 * 2 * N * N * N
 BYTES = 2 * (2048 * 512 + 2048 * 16) + (1024 * 512 + 1024 * 16) + 5 * N * N * 4 + 1024 * 4 + 3 * P * LIST_COLS * 2
@@ -81,12 +82,13 @@ def tile_picked_ymionet_err_p_kernel(
                 nc.vector.tensor_copy(t[:, h * HALF : (h + 1) * HALF], window.indirect(offsets[:, h * cols : (h + 1) * cols]))
             return t
 
-        def cast_weight(name, raw):
-            t = sb(name, [P, PACK * N], BF16, name)
-            nc.scalar.copy(
-                t[:].rearrange("p (t m j) -> p m j t", t=PACK, j=PACK),
-                raw[:].rearrange("p j (m t) -> p m j t", t=PACK),
-            )
+        def cast_weight(name, raw, groups):
+            t = sb(name, [P, PACK * N], BF16)
+            dealt = t[:].rearrange("p (t m j) -> p m j t", t=PACK, j=PACK)
+            rows = raw[:].rearrange("p j (m t) -> p m j t", t=PACK)
+            nc.scalar.copy(dealt[:, 0:groups], rows[:, 0:groups])
+            if groups < P:
+                nc.vector.tensor_copy(dealt[:, groups:P], rows[:, groups:P])
             return t
 
         def quantize(name, values, tag=None):
@@ -124,6 +126,8 @@ def tile_picked_ymionet_err_p_kernel(
         planes = sb("planes", [P, 2 * N], U8)
         nc.vector.memset(planes[:].bitcast(I32), 0)
         es, vs = (planes[:, i * N : (i + 1) * N] for i in range(2))
+        ident = sb("ident", [P, P], F32)
+        nc.vector.memset(ident[:], 0.0)
 
         w1_raw = load_weight("w1_raw", w1, nc.sync)
         offs_t = load_list("offs_t", offs)
@@ -150,17 +154,16 @@ def tile_picked_ymionet_err_p_kernel(
         ):
             tiles[b] = load_rows("%s%d" % (name, b), src, b)
 
-        ident = sb("ident", [P, P], F32)
-        make_identity(nc, ident[:])
+        make_identity(nc, ident[:], nomemset=True)
 
-        w1_bf = cast_weight("w1_bf", w1_raw)
+        w1_bf = cast_weight("w1_bf", w1_raw, SCALAR_GROUPS)
         w1_q = quantize("w1", w1_bf, "es_tab")
         phi_row = sb("phi_row", [P, N], F32)
         nc.scalar.activation(phi_row[:], phi_tab[:].indirect(pts_t[:]), ACT.Copy)
         phi_bank = bank_tile(2 * BLOCKS - 1)
         for c in range(BLOCKS):
             nc.tensor.transpose(phi_bank[:, c, :], phi_row[:, c * P : (c + 1) * P], ident[:])
-        w2_bf = cast_weight("w2_bf", w2_raw)
+        w2_bf = cast_weight("w2_bf", w2_raw, P)
         phi_col = sb("phi_col", [P, BLOCKS], F32, "w2_raw")
         nc.scalar.copy(phi_col[:], phi_bank[:, :, 0])
         xg = gather_halves("xg", x_tab[:].bitcast(U32), offs_t)

@@ -263,7 +263,6 @@ def tile_picked_ymionet_err_p_kernel(
         gap2 = sb("gap2", [P, N], F32, "z%d" % LAST)
         nc.gpsimd.tensor_tensor(gap2[:], lift_t[2][:], obs_t[2][:], ALU.subtract)
         gap3 = sb("gap3", [P, N], F32)
-        nc.gpsimd.tensor_tensor(gap3[:, 0:HALF], lift_t[LAST][:, 0:HALF], obs_t[LAST][:, 0:HALF], ALU.subtract)
         times_phi = []
         for i in range(2):
             times_phi.append(sb("times_phi%d" % i, [P, N], F32))
@@ -273,7 +272,7 @@ def tile_picked_ymionet_err_p_kernel(
             turn(back[j], columns(boundary[j]), start=True)
             turn(back[j], [t[:, j * P : (j + 1) * P] for t in scaled], stop=True)
         square_and_store(0, flat(back[0]), slice(0, N), nc.sync)
-        nc.vector.tensor_tensor(gap3[:, HALF:N], lift_t[LAST][:, HALF:N], obs_t[LAST][:, HALF:N], ALU.subtract)
+        nc.vector.tensor_tensor(gap3[:], lift_t[LAST][:], obs_t[LAST][:], ALU.subtract)
         for i, gap in enumerate((gap2, gap3)):
             err = sb("err%d" % (2 + i), [P, N], F32)
             nc.vector.tensor_tensor(err[:], times_phi[i][:], gap[:], ALU.add)

from contextlib import ExitStack

import concourse.mybir as mybir
from concourse.masks import make_identity

F32 = mybir.dt.float32
BF16 = mybir.dt.bfloat16
I32 = mybir.dt.int32
U32 = mybir.dt.uint32
U16 = mybir.dt.uint16
U8 = mybir.dt.uint8
FP8X4 = mybir.dt.float8_e4m3fn_x4
ALU = mybir.AluOpType
ACT = mybir.ActivationFunctionType

P = 128
PACK = 4
N = 512
BLOCKS = N // P
HALF = N // 2
LIST_COLS = N // 16
LAST = BLOCKS - 1
SPREAD = 8
SCALAR_GROUPS = 96

FLOPS = 3 * 2 * N * N * N
BYTES = 2 * (2048 * 512 + 2048 * 16) + (1024 * 512 + 1024 * 16) + 5 * N * N * 4 + 1024 * 4 + 3 * P * LIST_COLS * 2


def tile_picked_ymionet_err_p_kernel(
    tc, x_words, x_scales, e_words, e_scales, w1, w2, v_words, v_scales, phi, lift, obs, offs, coef, pts, out
):
    nc = tc.nc
    with ExitStack() as ctx:
        keep = ctx.enter_context(tc.tile_pool(name="keep", bufs=1))
        psum = ctx.enter_context(tc.psum_pool(name="psum", bufs=1))

        def sb(name, shape, dtype, tag=None, bufs=1):
            return keep.tile(shape, dtype, name=name, tag=tag or name, bufs=bufs, align_bytes=64)

        def load_list(name, src):
            t = keep.tile([P, LIST_COLS], U16, name=name)
            nc.sync.dma_start(t[:], src)
            return t

        def clear_scales(engine, name, src):
            t = sb(name, [P, src.shape[2]], U8)
            engine.memset(t[:].bitcast(I32), 0)
            return t

        def load_scales(t, src):
            nc.sync.dma_start(t[:].bitcast(I32)[0:P:SPREAD, :], src[0].bitcast(I32))

        def place_scales(dst, src):
            for r in range(PACK):
                nc.sync.dma_start(dst[:].bitcast(I32)[r:P:32, :], src[:].bitcast(I32)[SPREAD * r : P : 32, :])

        def load_words(name, src, tag=None):
            t = sb(name, [P, src.shape[2]], I32, tag)
            nc.sync.dma_start(t[:], src[0].rearrange("p n t -> p (n t)").bitcast(I32))
            return t

        def load_weight(name, src, queue):
            t = sb(name, [P, PACK, N], F32)
            queue.dma_start(t[:], src.rearrange("(p j) c -> p j c", j=PACK))
            return t

        def load_rows(name, src, b):
            t = sb(name, [P, N], F32)
            nc.sync.dma_start(t[:], src[b * P : (b + 1) * P, :])
            return t

        def gather(name, window, offsets, dtype, tag=None):
            t = sb(name, [P, N], dtype, tag)
            nc.vector.tensor_copy(t[:], window.indirect(offsets))
            return t

        def gather_halves(name, window, offsets, tag=None):
            t = sb(name, [P, N], U32, tag)
            cols = LIST_COLS // 2
            for h in range(2):
                nc.vector.tensor_copy(t[:, h * HALF : (h + 1) * HALF], window.indirect(offsets[:, h * cols : (h + 1) * cols]))
            return t

        def cast_weight(name, raw, groups):
            t = sb(name, [P, PACK * N], BF16)
            dealt = t[:].rearrange("p (t m j) -> p m j t", t=PACK, j=PACK)
            rows = raw[:].rearrange("p j (m t) -> p m j t", t=PACK)
            nc.scalar.copy(dealt[:, 0:groups], rows[:, 0:groups])
            if groups < P:
                nc.vector.tensor_copy(dealt[:, groups:P], rows[:, groups:P])
            return t

        def quantize(name, values, tag=None):
            width = values.shape[1] // PACK
            codes = sb(name + "_codes", [P, width], U32, tag)
            scales = sb(name + "_scales", [P, width], U8)
            nc.vector.quantize_mx(out=codes[:].bitcast(FP8X4), scales=scales[:], in_=values[:])
            return codes, scales

        def bank_tile(tag):
            return psum.tile([P, PACK, P], F32, name="bank%d" % tag)

        def branch(weight, words, scales, b, tag):
            codes, w_scales = weight
            bank = bank_tile(tag)
            for t in range(PACK):
                nc.tensor.matmul_mx(
                    out=bank[:, t, :],
                    lhsT=codes[:, t * P : (t + 1) * P].bitcast(FP8X4),
                    lhsT_scale=w_scales[:, t * P : (t + 1) * P],
                    rhs=words[:, b * P : (b + 1) * P].bitcast(FP8X4),
                    rhs_scale=scales[:, b * P : (b + 1) * P],
                    start=True,
                    stop=True,
                )
            return bank[:].rearrange("p t n -> p n t")

        xs_tab = clear_scales(nc.vector, "xs_tab", x_scales)
        es_tab = clear_scales(nc.vector, "es_tab", e_scales)
        phi_tab = sb("phi_tab", [P, phi.shape[1]], F32)
        nc.vector.memset(phi_tab[:], 0.0)
        vs_tab = clear_scales(nc.vector, "vs_tab", v_scales)
        xs = sb("xs", [P, N], U8)
        nc.vector.memset(xs[:].bitcast(I32), 0)
        planes = sb("planes", [P, 2 * N], U8)
        nc.vector.memset(planes[:].bitcast(I32), 0)
        es, vs = (planes[:, i * N : (i + 1) * N] for i in range(2))
        ident = sb("ident", [P, P], F32)
        nc.vector.memset(ident[:], 0.0)

        w1_raw = load_weight("w1_raw", w1, nc.sync)
        offs_t = load_list("offs_t", offs)
        load_scales(xs_tab, x_scales)
        coef_t = load_list("coef_t", coef)
        load_scales(es_tab, e_scales)
        pts_t = load_list("pts_t", pts)
        nc.sync.dma_start(phi_tab[0:1, :], phi[0:1, :])
        w2_raw = load_weight("w2_raw", w2, nc.sync)
        load_scales(vs_tab, v_scales)
        x_tab = load_words("x_tab", x_words)
        xs_rows = gather("xs_rows", xs_tab[:], offs_t[:], U8)
        place_scales(xs, xs_rows)
        e_tab = load_words("e_tab", e_words)
        v_tab = load_words("v_tab", v_words)
        scale_rows = sb("scale_rows", [P, 2 * N], U8)
        for i, (tab, offsets) in enumerate(((es_tab, coef_t), (vs_tab, pts_t))):
            nc.vector.tensor_copy(scale_rows[:, i * N : (i + 1) * N], tab[:].indirect(offsets[:]))
        place_scales(planes, scale_rows)
        obs_t, lift_t = {}, {}
        for tiles, name, src, b in (
            (obs_t, "obs", obs, 0), (obs_t, "obs", obs, 1), (lift_t, "lift", lift, 0), (obs_t, "obs", obs, 2),
            (lift_t, "lift", lift, 2), (obs_t, "obs", obs, 3), (lift_t, "lift", lift, 3), (lift_t, "lift", lift, 1),
        ):
            tiles[b] = load_rows("%s%d" % (name, b), src, b)

        make_identity(nc, ident[:], nomemset=True)

        w1_bf = cast_weight("w1_bf", w1_raw, SCALAR_GROUPS)
        w1_q = quantize("w1", w1_bf, "es_tab")
        phi_row = sb("phi_row", [P, N], F32)
        nc.scalar.activation(phi_row[:], phi_tab[:].indirect(pts_t[:]), ACT.Copy)
        phi_bank = bank_tile(2 * BLOCKS - 1)
        for c in range(BLOCKS):
            nc.tensor.transpose(phi_bank[:, c, :], phi_row[:, c * P : (c + 1) * P], ident[:])
        w2_bf = cast_weight("w2_bf", w2_raw, P)
        phi_col = sb("phi_col", [P, BLOCKS], F32, "w2_raw")
        nc.scalar.copy(phi_col[:], phi_bank[:, :, 0])
        xg = gather_halves("xg", x_tab[:].bitcast(U32), offs_t)
        w2_q = quantize("w2", w2_bf, "x_tab")

        y = []
        for b in range(BLOCKS):
            bank = branch(w1_q, xg, xs, b, b)
            t = sb("y%d" % b, [P, P, PACK], F32)
            nc.scalar.copy(t[:], bank)
            y.append(t)

        spread_bank = bank_tile(0)
        for c in range(BLOCKS):
            nc.tensor.transpose(spread_bank[:, c, :], phi_col[:, c : c + 1].to_broadcast([P, P]), ident[:])
        phi_full = sb("phi_full", [P, N], F32)
        nc.scalar.copy(phi_full[:], spread_bank[:].rearrange("p c n -> p (c n)"))

        eg = gather_halves("eg", e_tab[:].bitcast(U32), coef_t)
        vg = gather("vg", v_tab[:].bitcast(U32), pts_t[:], U32)
        u = [branch(w2_q, eg, es, b, BLOCKS + b) for b in range(BLOCKS)]

        def flat(bank):
            return bank[:].rearrange("p c n -> p (c n)")

        def turn(bank, src, start=False, stop=False):
            for c in range(BLOCKS):
                nc.tensor.matmul(
                    bank[:, c, :], src[c], ident[:], start=start and c == 0, stop=stop and c == LAST, is_transpose=True
                )

        def columns(t):
            return [t[:, c * P : (c + 1) * P] for c in range(BLOCKS)]

        def product(b):
            t = sb("z%d" % b, [P, P * PACK], BF16, "z0" if b == 2 else None)
            nc.vector.tensor_tensor(t[:].rearrange("p (n t) -> p n t", t=PACK), y[b][:], u[b], ALU.mult)
            return t

        def trunk(z_q, there):
            bank = bank_tile(there)
            nc.tensor.matmul_mx(
                out=flat(bank),
                lhsT=z_q[0][:].bitcast(FP8X4),
                lhsT_scale=z_q[1][:],
                rhs=vg[:].bitcast(FP8X4),
                rhs_scale=vs,
                start=True,
                stop=True,
            )
            return flat(bank)

        def square_and_store(b, total, cols, queue):
            res = sb("res%d_%d" % (b, cols.start), [P, cols.stop - cols.start], F32)
            nc.scalar.activation(res[:], total[:, cols], ACT.Square)
            queue.dma_start(out[b * P : (b + 1) * P, cols], res[:])

        minus_obs0 = sb("minus_obs0", [P, N], F32)
        nc.gpsimd.tensor_scalar(minus_obs0[:], obs_t[0][:], -1.0, 0.0, ALU.mult, ALU.add)
        edge = [bank_tile(2), bank_tile(3)]
        boundary = [sb("turned%d" % j, [P, N], F32) for j in range(2)]
        turn(edge[1], columns(obs_t[1]), start=True, stop=True)
        nc.scalar.activation(boundary[1][:], flat(edge[1]), ACT.Copy, scale=-1.0)
        turn(edge[0], columns(minus_obs0), start=True)
        turn(edge[0], columns(lift_t[0]), stop=True)
        nc.scalar.copy(boundary[0][:], flat(edge[0]))

        z = [product(0), product(1)]
        pair_codes = sb("pair_codes", [P, HALF], U32)
        pair_scales = sb("pair_scales", [P, HALF], U8)
        for i in range(2):
            cols = slice(i * P, (i + 1) * P)
            nc.vector.quantize_mx(out=pair_codes[:, cols].bitcast(FP8X4), scales=pair_scales[:, cols], in_=z[i][:])
        turned_trunk = []
        for c, there in enumerate((0, 0, 1, BLOCKS + 1)):
            if c != 1:
                bank = psum.tile([P, 2, HALF], F32, name="bank%d" % there)
            turned_trunk.append(bank[:, c % 2, :])
            nc.tensor.matmul_mx(
                out=turned_trunk[c],
                lhsT=vg[:, c * P : (c + 1) * P].bitcast(FP8X4),
                lhsT_scale=vs[:, c * P : (c + 1) * P],
                rhs=pair_codes[:].bitcast(FP8X4),
                rhs_scale=pair_scales[:],
                start=True,
                stop=True,
            )
        scaled = []
        for c in range(LAST):
            scaled.append(sb("scaled_chunk%d" % c, [P, HALF], F32))
            nc.scalar.activation(scaled[c][:], turned_trunk[c], ACT.Copy, scale=phi_col[:, c : c + 1])
        z = [product(2), product(3)]
        z_q = [quantize("z%d" % (2 + i), z[i]) for i in range(2)]
        ss = [trunk(z_q[i], BLOCKS + 2 + i) for i in range(2)]
        scaled.append(sb("scaled_chunk%d" % LAST, [P, HALF], F32, "z0"))
        nc.vector.tensor_scalar(scaled[LAST][:], turned_trunk[LAST], phi_col[:, LAST:BLOCKS], None, ALU.mult)
        gap2 = sb("gap2", [P, N], F32, "z%d" % LAST)
        nc.gpsimd.tensor_tensor(gap2[:], lift_t[2][:], obs_t[2][:], ALU.subtract)
        gap3 = sb("gap3", [P, N], F32)
        times_phi = []
        for i in range(2):
            times_phi.append(sb("times_phi%d" % i, [P, N], F32))
            nc.vector.tensor_tensor(times_phi[i][:], phi_full[:], ss[i], ALU.mult)
        back = [bank_tile(BLOCKS + 1), bank_tile(1)]
        for j in range(2):
            turn(back[j], columns(boundary[j]), start=True)
            turn(back[j], [t[:, j * P : (j + 1) * P] for t in scaled], stop=True)
        square_and_store(0, flat(back[0]), slice(0, N), nc.sync)
        nc.vector.tensor_tensor(gap3[:], lift_t[LAST][:], obs_t[LAST][:], ALU.subtract)
        for i, gap in enumerate((gap2, gap3)):
            err = sb("err%d" % (2 + i), [P, N], F32)
            nc.vector.tensor_tensor(err[:], times_phi[i][:], gap[:], ALU.add)
            square_and_store(2 + i, err, slice(0, N), nc.sync)
        err1 = sb("err1", [P, N], F32)
        for at in (0, HALF):
            cols = slice(at, at + HALF)
            nc.vector.tensor_tensor(err1[:, cols], lift_t[1][:, cols], flat(back[1])[:, cols], ALU.add)
            square_and_store(1, err1, cols, nc.scalar if at else nc.sync)
